import numpy as np
import ml_dtypes


def mxq(x, axis, fmt="e4m3"):
    dtype, down = {"e4m3": (ml_dtypes.float8_e4m3fn, 7), "e5m2": (ml_dtypes.float8_e5m2, 14)}[fmt]
    v = np.moveaxis(np.asarray(x, np.float32).astype(ml_dtypes.bfloat16).astype(np.float64), axis, -1)
    blocks = v.reshape(v.shape[:-1] + (-1, 32))
    amax = np.abs(blocks).max(-1, keepdims=True)
    byte = np.maximum(np.where(amax > 0, np.frexp(amax)[1] - 1 + 127, 0) - down, 1)
    scale = np.exp2(byte - 127.0)
    codes = (blocks / scale).astype(np.float32).astype(dtype).astype(np.float64)
    return np.moveaxis((codes * scale).reshape(v.shape), -1, axis)


WIDE = False


def mx_kscale(k):
    if not WIDE:
        return np.ones(k)
    levels = np.array([10, -10, 5, -5, 0])
    if k % 512:
        return np.exp2(np.random.permutation(np.resize(levels, k // 32))).repeat(32)
    a = np.empty((k // 512, 16))
    for p in range(k // 512):
        a[p, :8] = np.random.permutation(np.resize(levels, 8))
        for g in range(8):
            far = levels[np.abs(levels - a[p, g]) >= 10]
            a[p, g + 8] = far[np.random.randint(len(far))]
    return np.exp2(a.ravel()).repeat(32)


def f64(x):
    return np.asarray(x).astype(np.float64)


def striped(idx):
    return np.tile(idx.reshape(-1, 16).T, (8, 1)).astype(np.uint16)


def unstriped(offs):
    return offs[:16].T.reshape(-1).astype(np.int64)


def pack_weight(w):
    k, n = w.shape
    w = f64(np.asarray(w, np.float32).astype(ml_dtypes.bfloat16)).reshape(k // 32, 32, n)
    amax = np.abs(w).max(1)
    byte = np.clip(np.where(amax > 0, np.frexp(amax)[1] - 1 + 127 - 7, 1), 1, 254)
    scaled = (w * np.exp2(127.0 - byte)[:, None, :]).reshape(k, n).astype(np.float32)
    words = np.ascontiguousarray(scaled.reshape(k // 512, 128, 4, n).transpose(0, 1, 3, 2)).astype(ml_dtypes.float8_e4m3fn).view(np.uint8)
    return words, np.ascontiguousarray(byte.astype(np.uint8).reshape(k // 512, 16, n))


def unpack_weight(words, scales):
    g, p, n, _ = words.shape
    vals = np.ascontiguousarray(words).view(ml_dtypes.float8_e4m3fn).astype(np.float64) * np.repeat(np.exp2(scales.astype(np.float64) - 127.0), 8, axis=1)[..., None]
    return vals.transpose(0, 1, 3, 2).reshape(g * 512, n)


K, T, S, V, R = 1024, 2048, 512, 512, 256


def setup_inputs():
    n = np.random.standard_normal
    s = mx_kscale(K)[:, None]
    packed_xT = pack_weight(n((K, T)) * s)
    return {
        "x_words": packed_xT[0],
        "x_scales": packed_xT[1],
        "hT": (n((K, V)) / np.sqrt(K) / s).astype(np.float32),
        "att": (np.random.uniform(0.0, 1.0, (V, R)) ** 4 / R * 5).astype(np.float32),
        "cpw": (np.random.uniform(0.2, 0.8, (V, 1))).astype(np.float32),
        "gen": (np.random.uniform(0.2, 0.8, (V, 1))).astype(np.float32),
        "offs": striped(np.random.permutation(T)[:S]),
        "src": striped(np.random.permutation(S)[:R]),
    }


def reference(x_words, x_scales, hT, att, cpw, gen, offs, src):
    hTq = mxq(f64(hT), 0, "e4m3")
    xq = unpack_weight(x_words, x_scales)[:, unstriped(offs)]
    y = hTq.T @ xq
    ex = np.exp(y - y.max(axis=1, keepdims=True))
    p = ex / ex.sum(axis=1, keepdims=True)
    cp = np.zeros((S, S))
    cp[:, unstriped(src)] = f64(cpw) * f64(att)
    return f64(gen) * p + cp

@@ -1,0 +1,129 @@
+from contextlib import ExitStack
+
+import concourse.mybir as mybir
+
+K, T, S, V, R = 1024, 2048, 512, 512, 256
+FLOPS = 2 * K * V * S
+
+F32 = mybir.dt.float32
+BF16 = mybir.dt.bfloat16
+I32 = mybir.dt.int32
+U32 = mybir.dt.uint32
+U16 = mybir.dt.uint16
+U8 = mybir.dt.uint8
+FP8X4 = mybir.dt.float8_e4m3fn_x4
+ACT = mybir.ActivationFunctionType
+ALU = mybir.AluOpType
+
+P = 128
+PACK = 4
+K_PASS = P * PACK
+PASSES = K // K_PASS
+TILES = V // P
+HALF = V // 2
+
+
+def tile_picked_ycopy_mix_p_kernel(tc, x_words, x_scales, hT, att, cpw, gen, offs, src, out):
+    nc = tc.nc
+    with ExitStack() as ctx:
+        keep = ctx.enter_context(tc.tile_pool(name="keep", bufs=1))
+        psum = ctx.enter_context(tc.psum_pool(name="psum", bufs=1))
+
+        src_list = keep.tile([P, R // 16], U16, name="src_list")
+        offs_list = keep.tile([P, S // 16], U16, name="offs_list")
+        cpw_cols = keep.tile([P, TILES], F32, name="cpw_cols")
+        gen_cols = keep.tile([P, TILES], F32, name="gen_cols")
+        att_first = keep.tile([P, 1, R], F32, name="att_first")
+        att_rest = keep.tile([P, TILES - 1, R], F32, name="att_rest")
+        table_scales = keep.tile([P, T // 4], I32, name="table_scales")
+        table_words = [keep.tile([P, T], I32, name="table_words%d" % o) for o in range(PASSES)]
+        h_raw = [keep.tile([P, PACK, V], F32, name="h_raw%d" % o) for o in range(PASSES)]
+        copied = [keep.tile([P, S], F32, name="copied%d" % i) for i in range(TILES)]
+
+        zero = keep.tile([P, 1], F32, name="zero")
+        nc.vector.memset(zero[:], 0.0)
+        nc.vector.memset(table_scales[:], 0)
+        for i in range(TILES - 1):
+            nc.vector.memset(copied[i][:], 0.0)
+        nc.scalar.activation(copied[TILES - 1][:], zero[:].to_broadcast([P, S]), ACT.Copy)
+
+        att_view = att.rearrange("(i p) r -> p i r", p=P)
+        nc.sync.dma_start(src_list[:], src)
+        with nc.allow_non_contiguous_dma(reason="one value a partition and tile"):
+            nc.scalar.dma_start(cpw_cols[:], cpw.rearrange("(i p) o -> p (i o)", p=P))
+        nc.sync.dma_start(att_first[:], att_view[:, 0:1, :])
+        nc.sync.dma_start(offs_list[:], offs)
+        nc.sync.dma_start(att_rest[:], att_view[:, 1:TILES, :])
+        scale_words = x_scales.bitcast(I32)
+        for o in range(PASSES):
+            rows = hT[o * K_PASS : (o + 1) * K_PASS, :]
+            nc.sync.dma_start(h_raw[o][:], rows.rearrange("(p j) t -> p j t", j=PACK))
+            if o == 0:
+                for q in range(4):
+                    nc.sync.dma_start(table_scales[32 * q : 32 * q + 4 * PASSES, :], scale_words[:, 4 * q : 4 * q + 4, :])
+            nc.sync.dma_start(table_words[o][:], x_words[o].rearrange("p c r -> p (c r)").bitcast(I32))
+        with nc.allow_non_contiguous_dma(reason="one value a partition and tile"):
+            nc.sync.dma_start(gen_cols[:], gen.rearrange("(i p) o -> p (i o)", p=P))
+
+        nc.vector.tensor_copy(copied[0][:].indirect(src_list[:]), att_first[:, 0, :])
+        first_cp = keep.tile([P, S], F32, name="first_cp")
+        nc.scalar.activation(first_cp[:], copied[0][:], ACT.Copy, scale=cpw_cols[:, 0:1])
+        cp = [first_cp]
+        for i in range(1, TILES):
+            weighted = keep.tile([P, R], F32, name="weighted%d" % i)
+            nc.scalar.activation(weighted[:], att_rest[:, i - 1, :], ACT.Copy, scale=cpw_cols[:, i : i + 1])
+            nc.vector.tensor_copy(copied[i][:].indirect(src_list[:]), weighted[:])
+            cp.append(copied[i])
+
+        h_codes, h_scales = [], []
+        for o in range(PASSES):
+            codes = keep.tile([P, V], U32, name="h_codes%d" % o, align_bytes=64)
+            scales = keep.tile([P, V], U8, name="h_scales%d" % o, align_bytes=64)
+            for half in range(2):
+                cols = slice(half * HALF, (half + 1) * HALF)
+                grouped = keep.tile([P, HALF, PACK], BF16, name="grouped%d_%d" % (o, half), align_bytes=64)
+                nc.scalar.copy(
+                    grouped[:].rearrange("p (c i) j -> p c j i", i=4),
+                    h_raw[o][:, :, cols].rearrange("p j (c i) -> p c j i", i=4),
+                )
+                nc.vector.quantize_mx(
+                    out=codes[:, cols].bitcast(FP8X4), scales=scales[:, cols], in_=grouped[:].rearrange("p t j -> p (t j)")
+                )
+            h_codes.append(codes)
+            h_scales.append(scales)
+
+        x_planes = keep.tile([P, S], U8, name="x_planes", align_bytes=64)
+        nc.vector.tensor_copy(x_planes[:], table_scales[:].bitcast(U8).indirect(offs_list[:]))
+        banks = [psum.tile([P, S], F32, name="logits%d" % i) for i in range(TILES)]
+        for o in range(PASSES):
+            x_codes = keep.tile([P, S], U32, name="x_codes%d" % o, align_bytes=64)
+            nc.vector.tensor_copy(x_codes[:], table_words[o][:].bitcast(U32).indirect(offs_list[:]))
+            for i in range(TILES):
+                cols = slice(i * P, (i + 1) * P)
+                nc.tensor.matmul_mx(
+                    out=banks[i][:],
+                    lhsT=h_codes[o][:, cols].bitcast(FP8X4),
+                    lhsT_scale=h_scales[o][:, cols],
+                    rhs=x_codes[:].bitcast(FP8X4),
+                    rhs_scale=x_planes[4 * o : P, :],
+                    start=(o == 0),
+                    stop=(o == PASSES - 1),
+                )
+
+        exps, sums = [], []
+        for i in range(TILES):
+            minus_max = keep.tile([P, 1], F32, name="minus_max%d" % i)
+            nc.vector.tensor_reduce(minus_max[:], banks[i][:], mybir.AxisListType.X, ALU.max, negate=True)
+            e = keep.tile([P, S], F32, name="exp%d" % i)
+            total = keep.tile([P, 1], F32, name="total%d" % i)
+            nc.scalar.activation(e[:], banks[i][:], ACT.Exp, bias=minus_max[:], accum_out=total[:])
+            exps.append(e)
+            sums.append(total)
+        for i in range(TILES):
+            inverse = keep.tile([P, 1], F32, name="inverse%d" % i)
+            nc.vector.reciprocal(inverse[:], sums[i][:])
+            factor = keep.tile([P, 1], F32, name="factor%d" % i)
+            nc.vector.tensor_tensor(factor[:], inverse[:], gen_cols[:, i : i + 1], ALU.mult)
+            mixed = keep.tile([P, S], F32, name="mixed%d" % i)
+            nc.vector.scalar_tensor_tensor(mixed[:], exps[i][:], factor[:], cp[i][:], ALU.mult, ALU.add)
+            nc.sync.dma_start(out[i * P : (i + 1) * P, :], mixed[:])

@@ -21,6 +21,7 @@ K_PASS = P * PACK
 PASSES = K // K_PASS
 TILES = V // P
 HALF = V // 2
+LATE = R // 2
 
 
 def tile_picked_ycopy_mix_p_kernel(tc, x_words, x_scales, hT, att, cpw, gen, offs, src, out):
@@ -33,46 +34,53 @@ def tile_picked_ycopy_mix_p_kernel(tc, x_words, x_scales, hT, att, cpw, gen, off
         offs_list = keep.tile([P, S // 16], U16, name="offs_list")
         cpw_cols = keep.tile([P, TILES], F32, name="cpw_cols")
         gen_cols = keep.tile([P, TILES], F32, name="gen_cols")
-        att_first = keep.tile([P, 1, R], F32, name="att_first")
-        att_rest = keep.tile([P, TILES - 1, R], F32, name="att_rest")
+        att_first = keep.tile([P, R], F32, name="att_first")
+        att_rest = keep.tile([P, (TILES - 1) * R - LATE], F32, name="att_rest")
+        att_late = keep.tile([P, LATE], F32, name="att_late")
         table_scales = keep.tile([P, T // 4], I32, name="table_scales")
         table_words = [keep.tile([P, T], I32, name="table_words%d" % o) for o in range(PASSES)]
         h_raw = [keep.tile([P, PACK, V], F32, name="h_raw%d" % o) for o in range(PASSES)]
         copied = [keep.tile([P, S], F32, name="copied%d" % i) for i in range(TILES)]
 
         zero = keep.tile([P, 1], F32, name="zero")
+        nc.vector.memset(table_scales[:, : T // 8], 0)
+        nc.gpsimd.memset(table_scales[:, T // 8 :], 0)
         nc.vector.memset(zero[:], 0.0)
-        nc.vector.memset(table_scales[:], 0)
         for i in range(TILES - 1):
             nc.vector.memset(copied[i][:], 0.0)
         nc.scalar.activation(copied[TILES - 1][:], zero[:].to_broadcast([P, S]), ACT.Copy)
 
-        att_view = att.rearrange("(i p) r -> p i r", p=P)
+        att_view = att.rearrange("(p i) r -> p (i r)", i=TILES)
         nc.sync.dma_start(src_list[:], src)
-        with nc.allow_non_contiguous_dma(reason="one value a partition and tile"):
-            nc.scalar.dma_start(cpw_cols[:], cpw.rearrange("(i p) o -> p (i o)", p=P))
-        nc.sync.dma_start(att_first[:], att_view[:, 0:1, :])
+        nc.sync.dma_start(att_first[:], att_view[:, :R])
+        nc.sync.dma_start(cpw_cols[:], cpw.rearrange("(p i) o -> p (i o)", i=TILES))
+        nc.sync.dma_start(att_rest[:], att_view[:, R : TILES * R - LATE])
         nc.sync.dma_start(offs_list[:], offs)
-        nc.sync.dma_start(att_rest[:], att_view[:, 1:TILES, :])
+        nc.sync.dma_start(gen_cols[:], gen.rearrange("(p i) o -> p (i o)", i=TILES))
         scale_words = x_scales.bitcast(I32)
         for o in range(PASSES):
             rows = hT[o * K_PASS : (o + 1) * K_PASS, :]
             nc.sync.dma_start(h_raw[o][:], rows.rearrange("(p j) t -> p j t", j=PACK))
+            nc.sync.dma_start(table_words[o][:], x_words[o].rearrange("p c r -> p (c r)").bitcast(I32))
             if o == 0:
                 for q in range(4):
                     nc.sync.dma_start(table_scales[32 * q : 32 * q + 4 * PASSES, :], scale_words[:, 4 * q : 4 * q + 4, :])
-            nc.sync.dma_start(table_words[o][:], x_words[o].rearrange("p c r -> p (c r)").bitcast(I32))
-        with nc.allow_non_contiguous_dma(reason="one value a partition and tile"):
-            nc.sync.dma_start(gen_cols[:], gen.rearrange("(i p) o -> p (i o)", p=P))
+        nc.sync.dma_start(att_late[:], att_view[:, TILES * R - LATE :])
 
-        nc.vector.tensor_copy(copied[0][:].indirect(src_list[:]), att_first[:, 0, :])
+        nc.vector.tensor_copy(copied[0][:].indirect(src_list[:]), att_first[:])
         first_cp = keep.tile([P, S], F32, name="first_cp")
         nc.scalar.activation(first_cp[:], copied[0][:], ACT.Copy, scale=cpw_cols[:, 0:1])
         cp = [first_cp]
+
+        def scatter(i, values, first):
+            count = values.shape[1]
+            weighted = keep.tile([P, count], F32, name="weighted%d_%d" % (i, first))
+            nc.scalar.activation(weighted[:], values, ACT.Copy, scale=cpw_cols[:, i : i + 1])
+            places = src_list[:, first // 16 : (first + count) // 16]
+            nc.vector.tensor_copy(copied[i][:].indirect(places), weighted[:])
+
         for i in range(1, TILES):
-            weighted = keep.tile([P, R], F32, name="weighted%d" % i)
-            nc.scalar.activation(weighted[:], att_rest[:, i - 1, :], ACT.Copy, scale=cpw_cols[:, i : i + 1])
-            nc.vector.tensor_copy(copied[i][:].indirect(src_list[:]), weighted[:])
+            scatter(i, att_rest[:, (i - 1) * R : min(i * R, (TILES - 1) * R - LATE)], 0)
             cp.append(copied[i])
 
         h_codes, h_scales = [], []
@@ -83,8 +91,8 @@ def tile_picked_ycopy_mix_p_kernel(tc, x_words, x_scales, hT, att, cpw, gen, off
                 cols = slice(half * HALF, (half + 1) * HALF)
                 grouped = keep.tile([P, HALF, PACK], BF16, name="grouped%d_%d" % (o, half), align_bytes=64)
                 nc.scalar.copy(
-                    grouped[:].rearrange("p (c i) j -> p c j i", i=4),
-                    h_raw[o][:, :, cols].rearrange("p j (c i) -> p c j i", i=4),
+                    grouped[:].rearrange("p (i m) j -> p m j i", i=2),
+                    h_raw[o][:].rearrange("p j (m i) -> p m j i", i=TILES)[:, :, :, 2 * half : 2 * half + 2],
                 )
                 nc.vector.quantize_mx(
                     out=codes[:, cols].bitcast(FP8X4), scales=scales[:, cols], in_=grouped[:].rearrange("p t j -> p (t j)")
@@ -110,20 +118,23 @@ def tile_picked_ycopy_mix_p_kernel(tc, x_words, x_scales, hT, att, cpw, gen, off
                     stop=(o == PASSES - 1),
                 )
 
-        exps, sums = [], []
+        scatter(TILES - 1, att_late[:], R - LATE)
+
+        out_view = out.rearrange("(p i) j -> p i j", i=TILES)
+        exps, factors = [], []
         for i in range(TILES):
             minus_max = keep.tile([P, 1], F32, name="minus_max%d" % i)
             nc.vector.tensor_reduce(minus_max[:], banks[i][:], mybir.AxisListType.X, ALU.max, negate=True)
             e = keep.tile([P, S], F32, name="exp%d" % i)
             total = keep.tile([P, 1], F32, name="total%d" % i)
             nc.scalar.activation(e[:], banks[i][:], ACT.Exp, bias=minus_max[:], accum_out=total[:])
-            exps.append(e)
-            sums.append(total)
-        for i in range(TILES):
             inverse = keep.tile([P, 1], F32, name="inverse%d" % i)
-            nc.vector.reciprocal(inverse[:], sums[i][:])
+            nc.vector.reciprocal(inverse[:], total[:])
             factor = keep.tile([P, 1], F32, name="factor%d" % i)
-            nc.vector.tensor_tensor(factor[:], inverse[:], gen_cols[:, i : i + 1], ALU.mult)
+            nc.scalar.activation(factor[:], inverse[:], ACT.Copy, scale=gen_cols[:, i : i + 1])
+            exps.append(e)
+            factors.append(factor)
+        for i in range(TILES):
             mixed = keep.tile([P, S], F32, name="mixed%d" % i)
-            nc.vector.scalar_tensor_tensor(mixed[:], exps[i][:], factor[:], cp[i][:], ALU.mult, ALU.add)
-            nc.sync.dma_start(out[i * P : (i + 1) * P, :], mixed[:])
+            nc.vector.scalar_tensor_tensor(mixed[:], exps[i][:], factors[i][:], cp[i][:], ALU.mult, ALU.add)
+            nc.sync.dma_start(out_view[:, i, :], mixed[:])

@@ -20,14 +20,16 @@ PACK = 4
 K_PASS = P * PACK
 PASSES = K // K_PASS
 TILES = V // P
-HALF = V // 2
 LATE = R // 2
+H_PIECES = (1, 2)
+GROUPED = V * PACK * 2
 
 
 def tile_picked_ycopy_mix_p_kernel(tc, x_words, x_scales, hT, att, cpw, gen, offs, src, out):
     nc = tc.nc
     with ExitStack() as ctx:
         keep = ctx.enter_context(tc.tile_pool(name="keep", bufs=1))
+        reused = ctx.enter_context(tc.tile_pool(name="reused", bufs=1))
         psum = ctx.enter_context(tc.psum_pool(name="psum", bufs=1))
 
         src_list = keep.tile([P, R // 16], U16, name="src_list")
@@ -35,90 +37,89 @@ def tile_picked_ycopy_mix_p_kernel(tc, x_words, x_scales, hT, att, cpw, gen, off
         cpw_cols = keep.tile([P, TILES], F32, name="cpw_cols")
         gen_cols = keep.tile([P, TILES], F32, name="gen_cols")
         att_first = keep.tile([P, R], F32, name="att_first")
-        att_rest = keep.tile([P, (TILES - 1) * R - LATE], F32, name="att_rest")
-        att_late = keep.tile([P, LATE], F32, name="att_late")
-        table_scales = keep.tile([P, T // 4], I32, name="table_scales")
+        att_rest = keep.tile([P, TILES - 1, R], F32, name="att_rest")
+        table_scales = keep.tile([P, T // 4], I32, name="table_scales", tag="scales_then_h_codes", align_bytes=64)
         table_words = [keep.tile([P, T], I32, name="table_words%d" % o) for o in range(PASSES)]
-        h_raw = [keep.tile([P, PACK, V], F32, name="h_raw%d" % o) for o in range(PASSES)]
+        h_raw = [
+            [keep.tile([P, PACK, V // n], F32, name="h_raw%d_%d" % (o, c)) for c in range(n)] for o, n in enumerate(H_PIECES)
+        ]
         copied = [keep.tile([P, S], F32, name="copied%d" % i) for i in range(TILES)]
-
         zero = keep.tile([P, 1], F32, name="zero")
+
         nc.vector.memset(table_scales[:, : T // 8], 0)
         nc.gpsimd.memset(table_scales[:, T // 8 :], 0)
         nc.vector.memset(zero[:], 0.0)
-        for i in range(TILES - 1):
+        for i in range(TILES // 2):
             nc.vector.memset(copied[i][:], 0.0)
-        nc.scalar.activation(copied[TILES - 1][:], zero[:].to_broadcast([P, S]), ACT.Copy)
+        for i in range(TILES // 2, TILES):
+            nc.scalar.activation(copied[i][:], zero[:].to_broadcast([P, S]), ACT.Copy)
 
-        att_view = att.rearrange("(p i) r -> p (i r)", i=TILES)
+        att_view = att.rearrange("(p i) r -> p i r", i=TILES)
         nc.sync.dma_start(src_list[:], src)
-        nc.sync.dma_start(att_first[:], att_view[:, :R])
+        nc.sync.dma_start(att_first[:], att_view[:, 0, :])
         nc.sync.dma_start(cpw_cols[:], cpw.rearrange("(p i) o -> p (i o)", i=TILES))
-        nc.sync.dma_start(att_rest[:], att_view[:, R : TILES * R - LATE])
+        nc.sync.dma_start(att_rest[:], att_view[:, 1:, :])
         nc.sync.dma_start(offs_list[:], offs)
         nc.sync.dma_start(gen_cols[:], gen.rearrange("(p i) o -> p (i o)", i=TILES))
         scale_words = x_scales.bitcast(I32)
         for o in range(PASSES):
-            rows = hT[o * K_PASS : (o + 1) * K_PASS, :]
-            nc.sync.dma_start(h_raw[o][:], rows.rearrange("(p j) t -> p j t", j=PACK))
+            rows = hT[o * K_PASS : (o + 1) * K_PASS, :].rearrange("(p j) t -> p j t", j=PACK)
+            width = V // H_PIECES[o]
+            for c, piece in enumerate(h_raw[o]):
+                nc.sync.dma_start(piece[:], rows[:, :, c * width : (c + 1) * width])
             nc.sync.dma_start(table_words[o][:], x_words[o].rearrange("p c r -> p (c r)").bitcast(I32))
             if o == 0:
                 for q in range(4):
-                    nc.sync.dma_start(table_scales[32 * q : 32 * q + 4 * PASSES, :], scale_words[:, 4 * q : 4 * q + 4, :])
-        nc.sync.dma_start(att_late[:], att_view[:, TILES * R - LATE :])
+                    nc.gpsimd.dma_start(table_scales[32 * q : 32 * q + 4 * PASSES, :], scale_words[:, 4 * q : 4 * q + 4, :])
 
         nc.vector.tensor_copy(copied[0][:].indirect(src_list[:]), att_first[:])
         first_cp = keep.tile([P, S], F32, name="first_cp")
         nc.scalar.activation(first_cp[:], copied[0][:], ACT.Copy, scale=cpw_cols[:, 0:1])
-        cp = [first_cp]
+        cp = [first_cp] + copied[1:]
 
-        def scatter(i, values, first):
-            count = values.shape[1]
-            weighted = keep.tile([P, count], F32, name="weighted%d_%d" % (i, first))
+        def scatter(i, first, weighted):
+            count = weighted.shape[1]
+            values = att_rest[:, i - 1, first : first + count]
             nc.scalar.activation(weighted[:], values, ACT.Copy, scale=cpw_cols[:, i : i + 1])
             places = src_list[:, first // 16 : (first + count) // 16]
             nc.vector.tensor_copy(copied[i][:].indirect(places), weighted[:])
 
         for i in range(1, TILES):
-            scatter(i, att_rest[:, (i - 1) * R : min(i * R, (TILES - 1) * R - LATE)], 0)
-            cp.append(copied[i])
-
-        h_codes, h_scales = [], []
-        for o in range(PASSES):
-            codes = keep.tile([P, V], U32, name="h_codes%d" % o, align_bytes=64)
-            scales = keep.tile([P, V], U8, name="h_scales%d" % o, align_bytes=64)
-            for half in range(2):
-                cols = slice(half * HALF, (half + 1) * HALF)
-                grouped = keep.tile([P, HALF, PACK], BF16, name="grouped%d_%d" % (o, half), align_bytes=64)
-                nc.scalar.copy(
-                    grouped[:].rearrange("p (i m) j -> p m j i", i=2),
-                    h_raw[o][:].rearrange("p j (m i) -> p m j i", i=TILES)[:, :, :, 2 * half : 2 * half + 2],
-                )
-                nc.vector.quantize_mx(
-                    out=codes[:, cols].bitcast(FP8X4), scales=scales[:, cols], in_=grouped[:].rearrange("p t j -> p (t j)")
-                )
-            h_codes.append(codes)
-            h_scales.append(scales)
+            scatter(i, 0, keep.tile([P, R - LATE if i == TILES - 1 else R], F32, name="weighted%d" % i))
 
         x_planes = keep.tile([P, S], U8, name="x_planes", align_bytes=64)
-        nc.vector.tensor_copy(x_planes[:], table_scales[:].bitcast(U8).indirect(offs_list[:]))
         banks = [psum.tile([P, S], F32, name="logits%d" % i) for i in range(TILES)]
         for o in range(PASSES):
-            x_codes = keep.tile([P, S], U32, name="x_codes%d" % o, align_bytes=64)
+            grouped = reused.tile([P, TILES, P, PACK], BF16, name="grouped%d" % o, offset=o * GROUPED, align_bytes=64)
+            part = P // H_PIECES[o]
+            for c, piece in enumerate(h_raw[o]):
+                nc.scalar.copy(
+                    grouped[:, :, c * part : (c + 1) * part, :].rearrange("p i m j -> p m j i"),
+                    piece[:].rearrange("p j (m i) -> p m j i", i=TILES),
+                )
+            h_codes = keep.tile(
+                [P, V], U32, name="h_codes%d" % o, tag="h_codes0" if o == 0 else "scales_then_h_codes", align_bytes=64
+            )
+            h_scales = keep.tile([P, V], U8, name="h_scales%d" % o, align_bytes=64)
+            nc.vector.quantize_mx(
+                out=h_codes[:].bitcast(FP8X4), scales=h_scales[:], in_=grouped[:].rearrange("p i m j -> p (i m j)")
+            )
+            if o == 0:
+                nc.vector.tensor_copy(x_planes[:], table_scales[:].bitcast(U8).indirect(offs_list[:]))
+            x_codes = reused.tile([P, S], U32, name="x_codes%d" % o, offset=(2 - o) * GROUPED, align_bytes=64)
             nc.vector.tensor_copy(x_codes[:], table_words[o][:].bitcast(U32).indirect(offs_list[:]))
             for i in range(TILES):
                 cols = slice(i * P, (i + 1) * P)
                 nc.tensor.matmul_mx(
                     out=banks[i][:],
-                    lhsT=h_codes[o][:, cols].bitcast(FP8X4),
-                    lhsT_scale=h_scales[o][:, cols],
+                    lhsT=h_codes[:, cols].bitcast(FP8X4),
+                    lhsT_scale=h_scales[:, cols],
                     rhs=x_codes[:].bitcast(FP8X4),
                     rhs_scale=x_planes[4 * o : P, :],
                     start=(o == 0),
                     stop=(o == PASSES - 1),
                 )
-
-        scatter(TILES - 1, att_late[:], R - LATE)
+        scatter(TILES - 1, R - LATE, reused.tile([P, LATE], F32, name="weighted_late", offset=GROUPED + 4 * S))
 
         out_view = out.rearrange("(p i) j -> p i j", i=TILES)
         exps, factors = [], []

@@ -20,62 +20,58 @@ PACK = 4
 K_PASS = P * PACK
 PASSES = K // K_PASS
 TILES = V // P
+H_PIECES = ((0, P), (P, 2 * P), (2 * P, V))
 LATE = R // 2
-H_PIECES = (1, 2)
-GROUPED = V * PACK * 2
+PASS_BYTES = V * PACK * 4
 
 
 def tile_picked_ycopy_mix_p_kernel(tc, x_words, x_scales, hT, att, cpw, gen, offs, src, out):
     nc = tc.nc
     with ExitStack() as ctx:
         keep = ctx.enter_context(tc.tile_pool(name="keep", bufs=1))
-        reused = ctx.enter_context(tc.tile_pool(name="reused", bufs=1))
+        late = ctx.enter_context(tc.tile_pool(name="late", bufs=1))
         psum = ctx.enter_context(tc.psum_pool(name="psum", bufs=1))
 
         src_list = keep.tile([P, R // 16], U16, name="src_list")
         offs_list = keep.tile([P, S // 16], U16, name="offs_list")
         cpw_cols = keep.tile([P, TILES], F32, name="cpw_cols")
-        gen_cols = keep.tile([P, TILES], F32, name="gen_cols")
-        att_first = keep.tile([P, R], F32, name="att_first")
         att_rest = keep.tile([P, TILES - 1, R], F32, name="att_rest")
-        table_scales = keep.tile([P, T // 4], I32, name="table_scales", tag="scales_then_h_codes", align_bytes=64)
-        table_words = [keep.tile([P, T], I32, name="table_words%d" % o) for o in range(PASSES)]
-        h_raw = [
-            [keep.tile([P, PACK, V // n], F32, name="h_raw%d_%d" % (o, c)) for c in range(n)] for o, n in enumerate(H_PIECES)
-        ]
+        table_scales = keep.tile([P, T // 4], I32, name="table_scales")
         copied = [keep.tile([P, S], F32, name="copied%d" % i) for i in range(TILES)]
-        zero = keep.tile([P, 1], F32, name="zero")
+        zero = keep.tile([P, 1], F32, name="zero", tag="zero")
+        att_first = keep.tile([P, R], F32, name="att_first", tag="table_words0")
+        h_raw = [keep.tile([P, PACK, V], F32, name="h_raw0"), late.tile([P, PACK * V], F32, name="h_raw1", offset=0)]
+        gen_cols = keep.tile([P, TILES], F32, name="gen_cols", tag="zero")
+        table_words = [
+            keep.tile([P, T], I32, name="table_words0", tag="table_words0"),
+            late.tile([P, T], I32, name="table_words1", offset=PASS_BYTES),
+        ]
 
-        nc.vector.memset(table_scales[:, : T // 8], 0)
-        nc.gpsimd.memset(table_scales[:, T // 8 :], 0)
         nc.vector.memset(zero[:], 0.0)
+        nc.vector.memset(table_scales[:], 0)
         for i in range(TILES // 2):
             nc.vector.memset(copied[i][:], 0.0)
-        for i in range(TILES // 2, TILES):
-            nc.scalar.activation(copied[i][:], zero[:].to_broadcast([P, S]), ACT.Copy)
 
-        att_view = att.rearrange("(p i) r -> p i r", i=TILES)
+        att_view = att.rearrange("(i p) r -> p i r", p=P)
+        h_view = hT.rearrange("(o p j) t -> o p j t", p=P, j=PACK)
+        word_view = x_words.rearrange("o p c r -> o p (c r)").bitcast(I32)
+        scale_view = x_scales.bitcast(I32)
         nc.sync.dma_start(src_list[:], src)
         nc.sync.dma_start(att_first[:], att_view[:, 0, :])
-        nc.sync.dma_start(cpw_cols[:], cpw.rearrange("(p i) o -> p (i o)", i=TILES))
+        with nc.allow_non_contiguous_dma(reason="one value a partition and tile"):
+            nc.scalar.dma_start(cpw_cols[:], cpw.rearrange("(i p) o -> p (i o)", p=P))
         nc.sync.dma_start(att_rest[:], att_view[:, 1:, :])
         nc.sync.dma_start(offs_list[:], offs)
-        nc.sync.dma_start(gen_cols[:], gen.rearrange("(p i) o -> p (i o)", i=TILES))
-        scale_words = x_scales.bitcast(I32)
-        for o in range(PASSES):
-            rows = hT[o * K_PASS : (o + 1) * K_PASS, :].rearrange("(p j) t -> p j t", j=PACK)
-            width = V // H_PIECES[o]
-            for c, piece in enumerate(h_raw[o]):
-                nc.sync.dma_start(piece[:], rows[:, :, c * width : (c + 1) * width])
-            nc.sync.dma_start(table_words[o][:], x_words[o].rearrange("p c r -> p (c r)").bitcast(I32))
-            if o == 0:
-                for q in range(4):
-                    nc.gpsimd.dma_start(table_scales[32 * q : 32 * q + 4 * PASSES, :], scale_words[:, 4 * q : 4 * q + 4, :])
+        nc.sync.dma_start(h_raw[0][:], h_view[0])
+        for q in range(4):
+            nc.sync.dma_start(table_scales[32 * q : 32 * q + 4 * PASSES, :], scale_view[:, 4 * q : 4 * q + 4, :])
+        for i in range(TILES // 2, TILES):
+            nc.scalar.activation(copied[i][:], zero[:].to_broadcast([P, S]), ACT.Copy)
+        with nc.allow_non_contiguous_dma(reason="one value a partition and tile"):
+            nc.scalar.dma_start(gen_cols[:], gen.rearrange("(i p) o -> p (i o)", p=P))
 
         nc.vector.tensor_copy(copied[0][:].indirect(src_list[:]), att_first[:])
-        first_cp = keep.tile([P, S], F32, name="first_cp")
-        nc.scalar.activation(first_cp[:], copied[0][:], ACT.Copy, scale=cpw_cols[:, 0:1])
-        cp = [first_cp] + copied[1:]
+        nc.sync.dma_start(table_words[0][:], word_view[0])
 
         def scatter(i, first, weighted):
             count = weighted.shape[1]
@@ -84,49 +80,68 @@ def tile_picked_ycopy_mix_p_kernel(tc, x_words, x_scales, hT, att, cpw, gen, off
             places = src_list[:, first // 16 : (first + count) // 16]
             nc.vector.tensor_copy(copied[i][:].indirect(places), weighted[:])
 
-        for i in range(1, TILES):
-            scatter(i, 0, keep.tile([P, R - LATE if i == TILES - 1 else R], F32, name="weighted%d" % i))
+        scatter(1, 0, late.tile([P, R], F32, name="weighted1", offset=PASS_BYTES - 2 * R))
+        nc.sync.dma_start(table_words[1][:], word_view[1])
+        h_late = []
+        for first, last in H_PIECES:
+            piece = h_raw[1][:, PACK * first : PACK * last].rearrange("p (j t) -> p j t", j=PACK)
+            nc.sync.dma_start(piece, h_view[1][:, :, first:last])
+            h_late.extend(piece[:, :, t : t + P] for t in range(0, last - first, P))
+        scatter(2, 0, keep.tile([P, R], F32, name="weighted2"))
+        scatter(3, 0, keep.tile([P, R - LATE], F32, name="weighted3"))
 
-        x_planes = keep.tile([P, S], U8, name="x_planes", align_bytes=64)
+        def quantize(raw, name):
+            width = raw.shape[2]
+            grouped = keep.tile([P, width, PACK], BF16, name="grouped" + name, tag="grouped" + name, align_bytes=64)
+            nc.scalar.copy(
+                grouped[:].rearrange("p (c i) j -> p c j i", i=4),
+                raw.rearrange("p j (c i) -> p c j i", i=4),
+            )
+            codes = keep.tile([P, width], U32, name="h_codes" + name, align_bytes=64)
+            scales = keep.tile([P, width], U8, name="h_scales" + name, align_bytes=64)
+            nc.vector.quantize_mx(out=codes[:].bitcast(FP8X4), scales=scales[:], in_=grouped[:].rearrange("p t j -> p (t j)"))
+            return codes, scales
+
+        def gather_words(o):
+            codes = keep.tile([P, S], U32, name="x_codes%d" % o, align_bytes=64)
+            nc.vector.tensor_copy(codes[:], table_words[o][:].bitcast(U32).indirect(offs_list[:]))
+            return codes
+
         banks = [psum.tile([P, S], F32, name="logits%d" % i) for i in range(TILES)]
-        for o in range(PASSES):
-            grouped = reused.tile([P, TILES, P, PACK], BF16, name="grouped%d" % o, offset=o * GROUPED, align_bytes=64)
-            part = P // H_PIECES[o]
-            for c, piece in enumerate(h_raw[o]):
-                nc.scalar.copy(
-                    grouped[:, :, c * part : (c + 1) * part, :].rearrange("p i m j -> p m j i"),
-                    piece[:].rearrange("p j (m i) -> p m j i", i=TILES),
-                )
-            h_codes = keep.tile(
-                [P, V], U32, name="h_codes%d" % o, tag="h_codes0" if o == 0 else "scales_then_h_codes", align_bytes=64
-            )
-            h_scales = keep.tile([P, V], U8, name="h_scales%d" % o, align_bytes=64)
-            nc.vector.quantize_mx(
-                out=h_codes[:].bitcast(FP8X4), scales=h_scales[:], in_=grouped[:].rearrange("p i m j -> p (i m j)")
-            )
-            if o == 0:
-                nc.vector.tensor_copy(x_planes[:], table_scales[:].bitcast(U8).indirect(offs_list[:]))
-            x_codes = reused.tile([P, S], U32, name="x_codes%d" % o, offset=(2 - o) * GROUPED, align_bytes=64)
-            nc.vector.tensor_copy(x_codes[:], table_words[o][:].bitcast(U32).indirect(offs_list[:]))
-            for i in range(TILES):
-                cols = slice(i * P, (i + 1) * P)
-                nc.tensor.matmul_mx(
-                    out=banks[i][:],
-                    lhsT=h_codes[:, cols].bitcast(FP8X4),
-                    lhsT_scale=h_scales[:, cols],
-                    rhs=x_codes[:].bitcast(FP8X4),
-                    rhs_scale=x_planes[4 * o : P, :],
-                    start=(o == 0),
-                    stop=(o == PASSES - 1),
-                )
-        scatter(TILES - 1, R - LATE, reused.tile([P, LATE], F32, name="weighted_late", offset=GROUPED + 4 * S))
+        x_planes = keep.tile([P, S], U8, name="x_planes", align_bytes=64)
 
-        out_view = out.rearrange("(p i) j -> p i j", i=TILES)
+        def multiply(i, o, h_codes, h_scales, x_codes):
+            nc.tensor.matmul_mx(
+                out=banks[i][:],
+                lhsT=h_codes.bitcast(FP8X4),
+                lhsT_scale=h_scales,
+                rhs=x_codes[:].bitcast(FP8X4),
+                rhs_scale=x_planes[4 * o : P, :],
+                start=(o == 0),
+                stop=(o == PASSES - 1),
+            )
+
+        nc.vector.tensor_copy(x_planes[:], table_scales[:].bitcast(U8).indirect(offs_list[:]))
+        h_codes, h_scales = quantize(h_raw[0][:], "0")
+        x_codes = gather_words(0)
+        for i in range(TILES):
+            multiply(i, 0, h_codes[:, i * P : (i + 1) * P], h_scales[:, i * P : (i + 1) * P], x_codes)
+
+        scatter(TILES - 1, R - LATE, keep.tile([P, LATE], F32, name="weighted_late", tag="grouped0", align_bytes=64))
+        x_codes = gather_words(1)
+        for i in range(TILES):
+            h_codes, h_scales = quantize(h_late[i], "1_%d" % i)
+            multiply(i, 1, h_codes[:], h_scales[:], x_codes)
+        first_cp = keep.tile([P, S], F32, name="first_cp", tag="table_words0")
+        nc.scalar.activation(first_cp[:], copied[0][:], ACT.Copy, scale=cpw_cols[:, 0:1])
+        cp = [first_cp] + copied[1:]
+
         exps, factors = [], []
         for i in range(TILES):
-            minus_max = keep.tile([P, 1], F32, name="minus_max%d" % i)
+            tag = "grouped1_2" if i == 1 else "minus_max%d" % i
+            minus_max = keep.tile([P, 1], F32, name="minus_max%d" % i, tag=tag, align_bytes=64)
             nc.vector.tensor_reduce(minus_max[:], banks[i][:], mybir.AxisListType.X, ALU.max, negate=True)
-            e = keep.tile([P, S], F32, name="exp%d" % i)
+            e = late.tile([P, S], F32, name="exp%d" % i, offset=4 * S * i)
             total = keep.tile([P, 1], F32, name="total%d" % i)
             nc.scalar.activation(e[:], banks[i][:], ACT.Exp, bias=minus_max[:], accum_out=total[:])
             inverse = keep.tile([P, 1], F32, name="inverse%d" % i)
@@ -136,6 +151,9 @@ def tile_picked_ycopy_mix_p_kernel(tc, x_words, x_scales, hT, att, cpw, gen, off
             exps.append(e)
             factors.append(factor)
         for i in range(TILES):
-            mixed = keep.tile([P, S], F32, name="mixed%d" % i)
-            nc.vector.scalar_tensor_tensor(mixed[:], exps[i][:], factors[i][:], cp[i][:], ALU.mult, ALU.add)
-            nc.sync.dma_start(out_view[:, i, :], mixed[:])
+            width = S // 2 if i == TILES - 1 else S
+            for first in range(0, S, width):
+                cols = slice(first, first + width)
+                mixed = keep.tile([P, width], F32, name="mixed%d_%d" % (i, first))
+                nc.vector.scalar_tensor_tensor(mixed[:], exps[i][:, cols], factors[i][:], cp[i][:, cols], ALU.mult, ALU.add)
+                nc.sync.dma_start(out[i * P : (i + 1) * P, cols], mixed[:])

@@ -1,6 +1,7 @@
 from contextlib import ExitStack
 
 import concourse.mybir as mybir
+from concourse.masks import make_identity
 
 K, T, S, V, R = 1024, 2048, 512, 512, 256
 FLOPS = 2 * K * V * S
@@ -20,9 +21,14 @@ PACK = 4
 K_PASS = P * PACK
 PASSES = K // K_PASS
 TILES = V // P
-H_PIECES = ((0, P), (P, 2 * P), (2 * P, V))
+LAST = TILES - 1
 LATE = R // 2
-PASS_BYTES = V * PACK * 4
+ROWS_AT = P - 2 * TILES
+PIECE_BYTES = P * PACK * 4
+
+
+def place(i, o):
+    return (PASSES * i + o + (1 if (i, o) == (LAST, 1) else 0)) * PIECE_BYTES
 
 
 def tile_picked_ycopy_mix_p_kernel(tc, x_words, x_scales, hT, att, cpw, gen, offs, src, out):
@@ -30,130 +36,159 @@ def tile_picked_ycopy_mix_p_kernel(tc, x_words, x_scales, hT, att, cpw, gen, off
     with ExitStack() as ctx:
         keep = ctx.enter_context(tc.tile_pool(name="keep", bufs=1))
         late = ctx.enter_context(tc.tile_pool(name="late", bufs=1))
+        early = ctx.enter_context(tc.tile_pool(name="early", bufs=1))
         psum = ctx.enter_context(tc.psum_pool(name="psum", bufs=1))
 
         src_list = keep.tile([P, R // 16], U16, name="src_list")
         offs_list = keep.tile([P, S // 16], U16, name="offs_list")
-        cpw_cols = keep.tile([P, TILES], F32, name="cpw_cols")
-        att_rest = keep.tile([P, TILES - 1, R], F32, name="att_rest")
+        rows = keep.tile([P, P], F32, name="rows")
+        identity = keep.tile([P, P], F32, name="identity")
+        att_first = keep.tile([P, R], F32, name="att_first")
+        att_middle = early.tile([P, 2, R], F32, name="att_middle", offset=256)
+        att_last = keep.tile([P, R], F32, name="att_last")
         table_scales = keep.tile([P, T // 4], I32, name="table_scales")
         copied = [keep.tile([P, S], F32, name="copied%d" % i) for i in range(TILES)]
-        zero = keep.tile([P, 1], F32, name="zero", tag="zero")
-        att_first = keep.tile([P, R], F32, name="att_first", tag="table_words0")
-        h_raw = [keep.tile([P, PACK, V], F32, name="h_raw0"), late.tile([P, PACK * V], F32, name="h_raw1", offset=0)]
-        gen_cols = keep.tile([P, TILES], F32, name="gen_cols", tag="zero")
-        table_words = [
-            keep.tile([P, T], I32, name="table_words0", tag="table_words0"),
-            late.tile([P, T], I32, name="table_words1", offset=PASS_BYTES),
+        zero = keep.tile([P, 1], F32, name="zero")
+        table_words = [keep.tile([P, T], I32, name="table_words%d" % o) for o in range(PASSES)]
+        h_raw = [
+            [late.tile([P, PACK, P], F32, name="h_raw%d_%d" % (i, o), offset=place(i, o)) for o in range(PASSES)]
+            for i in range(TILES)
         ]
 
-        nc.vector.memset(zero[:], 0.0)
         nc.vector.memset(table_scales[:], 0)
-        for i in range(TILES // 2):
+        nc.vector.memset(rows[0:ROWS_AT, :], 0.0)
+        nc.vector.memset(zero[:], 0.0)
+        for i in range(LAST):
             nc.vector.memset(copied[i][:], 0.0)
+        make_identity(nc, identity[:])
 
         att_view = att.rearrange("(i p) r -> p i r", p=P)
         h_view = hT.rearrange("(o p j) t -> o p j t", p=P, j=PACK)
         word_view = x_words.rearrange("o p c r -> o p (c r)").bitcast(I32)
         scale_view = x_scales.bitcast(I32)
+        nc.scalar.dma_start(rows[ROWS_AT : ROWS_AT + TILES, :], cpw.rearrange("(i p) o -> i (p o)", p=P))
+        nc.scalar.dma_start(rows[ROWS_AT + TILES : P, :], gen.rearrange("(i p) o -> i (p o)", p=P))
         nc.sync.dma_start(src_list[:], src)
         nc.sync.dma_start(att_first[:], att_view[:, 0, :])
-        with nc.allow_non_contiguous_dma(reason="one value a partition and tile"):
-            nc.scalar.dma_start(cpw_cols[:], cpw.rearrange("(i p) o -> p (i o)", p=P))
-        nc.sync.dma_start(att_rest[:], att_view[:, 1:, :])
-        nc.sync.dma_start(offs_list[:], offs)
-        nc.sync.dma_start(h_raw[0][:], h_view[0])
+        nc.sync.dma_start(att_middle[:], att_view[:, 1:LAST, :])
+        nc.sync.dma_start(att_last[:], att_view[:, LAST, :])
+        nc.sync.dma_start(table_words[0][:], word_view[0])
         for q in range(4):
             nc.sync.dma_start(table_scales[32 * q : 32 * q + 4 * PASSES, :], scale_view[:, 4 * q : 4 * q + 4, :])
-        for i in range(TILES // 2, TILES):
-            nc.scalar.activation(copied[i][:], zero[:].to_broadcast([P, S]), ACT.Copy)
-        with nc.allow_non_contiguous_dma(reason="one value a partition and tile"):
-            nc.scalar.dma_start(gen_cols[:], gen.rearrange("(i p) o -> p (i o)", p=P))
+        nc.sync.dma_start(offs_list[:], offs)
+        nc.sync.dma_start(table_words[1][:], word_view[1])
+        for i in range(TILES):
+            for o in range(PASSES):
+                nc.sync.dma_start(h_raw[i][o][:], h_view[o][:, :, i * P : (i + 1) * P])
+
+        nc.scalar.activation(copied[LAST][:], zero[:].to_broadcast([P, S]), ACT.Copy)
+        turned = psum.tile([P, P], F32, name="turned")
+        nc.tensor.transpose(turned[:], rows[:], identity[:])
+        weights = keep.tile([P, 2 * TILES], F32, name="weights")
+        nc.scalar.copy(weights[:], turned[:, ROWS_AT:P])
 
         nc.vector.tensor_copy(copied[0][:].indirect(src_list[:]), att_first[:])
-        nc.sync.dma_start(table_words[0][:], word_view[0])
 
         def scatter(i, first, weighted):
             count = weighted.shape[1]
-            values = att_rest[:, i - 1, first : first + count]
-            nc.scalar.activation(weighted[:], values, ACT.Copy, scale=cpw_cols[:, i : i + 1])
+            values = (att_last if i == LAST else att_middle[:, i - 1, :])[:, first : first + count]
+            nc.scalar.activation(weighted[:], values, ACT.Copy, scale=weights[:, i : i + 1])
             places = src_list[:, first // 16 : (first + count) // 16]
             nc.vector.tensor_copy(copied[i][:].indirect(places), weighted[:])
 
-        scatter(1, 0, late.tile([P, R], F32, name="weighted1", offset=PASS_BYTES - 2 * R))
-        nc.sync.dma_start(table_words[1][:], word_view[1])
-        h_late = []
-        for first, last in H_PIECES:
-            piece = h_raw[1][:, PACK * first : PACK * last].rearrange("p (j t) -> p j t", j=PACK)
-            nc.sync.dma_start(piece, h_view[1][:, :, first:last])
-            h_late.extend(piece[:, :, t : t + P] for t in range(0, last - first, P))
+        scatter(1, 0, keep.tile([P, R], F32, name="weighted1", tag="weighted1"))
         scatter(2, 0, keep.tile([P, R], F32, name="weighted2"))
-        scatter(3, 0, keep.tile([P, R - LATE], F32, name="weighted3"))
+        scatter(LAST, 0, keep.tile([P, R - LATE], F32, name="weighted3"))
+        first_cp = keep.tile([P, S], F32, name="first_cp", tag="weighted1")
+        nc.scalar.activation(first_cp[:], copied[0][:], ACT.Copy, scale=weights[:, 0:1])
+        cp = [first_cp] + copied[1:]
 
-        def quantize(raw, name):
-            width = raw.shape[2]
-            grouped = keep.tile([P, width, PACK], BF16, name="grouped" + name, tag="grouped" + name, align_bytes=64)
-            nc.scalar.copy(
-                grouped[:].rearrange("p (c i) j -> p c j i", i=4),
-                raw.rearrange("p j (c i) -> p c j i", i=4),
-            )
+        x_planes = early.tile([P, S], U8, name="x_planes", align_bytes=64, offset=0)
+        nc.vector.tensor_copy(x_planes[:], table_scales[:].bitcast(U8).indirect(offs_list[:]))
+        x_codes = []
+        for o in range(PASSES):
+            codes = early.tile([P, S], U32, name="x_codes%d" % o, align_bytes=64, offset=S + 4 * S * o)
+            nc.vector.tensor_copy(codes[:], table_words[o][:].bitcast(U32).indirect(offs_list[:]))
+            x_codes.append(codes)
+
+        banks = [psum.tile([P, S], F32, name="logits%d" % i) for i in range(TILES)]
+
+        def multiply(i, passes):
+            name = "%d_%d" % (i, passes[0])
+            width = P * len(passes)
+            grouped = keep.tile([P, width, PACK], BF16, name="grouped" + name, align_bytes=64)
+            for n, o in enumerate(passes):
+                nc.scalar.copy(
+                    grouped[:, n * P : (n + 1) * P, :].rearrange("p (c i) j -> p c j i", i=4),
+                    h_raw[i][o][:].rearrange("p j (c i) -> p c j i", i=4),
+                )
             codes = keep.tile([P, width], U32, name="h_codes" + name, align_bytes=64)
             scales = keep.tile([P, width], U8, name="h_scales" + name, align_bytes=64)
             nc.vector.quantize_mx(out=codes[:].bitcast(FP8X4), scales=scales[:], in_=grouped[:].rearrange("p t j -> p (t j)"))
-            return codes, scales
+            for n, o in enumerate(passes):
+                nc.tensor.matmul_mx(
+                    out=banks[i][:],
+                    lhsT=codes[:, n * P : (n + 1) * P].bitcast(FP8X4),
+                    lhsT_scale=scales[:, n * P : (n + 1) * P],
+                    rhs=x_codes[o][:].bitcast(FP8X4),
+                    rhs_scale=x_planes[4 * o : P, :],
+                    start=(o == 0),
+                    stop=(o == PASSES - 1),
+                )
 
-        def gather_words(o):
-            codes = keep.tile([P, S], U32, name="x_codes%d" % o, align_bytes=64)
-            nc.vector.tensor_copy(codes[:], table_words[o][:].bitcast(U32).indirect(offs_list[:]))
-            return codes
+        def held(shape, name, i, o, first=0):
+            return late.tile(shape, F32, name=name, offset=place(i, o) + first)
 
-        banks = [psum.tile([P, S], F32, name="logits%d" % i) for i in range(TILES)]
-        x_planes = keep.tile([P, S], U8, name="x_planes", align_bytes=64)
+        maxima = {}
 
-        def multiply(i, o, h_codes, h_scales, x_codes):
-            nc.tensor.matmul_mx(
-                out=banks[i][:],
-                lhsT=h_codes.bitcast(FP8X4),
-                lhsT_scale=h_scales,
-                rhs=x_codes[:].bitcast(FP8X4),
-                rhs_scale=x_planes[4 * o : P, :],
-                start=(o == 0),
-                stop=(o == PASSES - 1),
-            )
-
-        nc.vector.tensor_copy(x_planes[:], table_scales[:].bitcast(U8).indirect(offs_list[:]))
-        h_codes, h_scales = quantize(h_raw[0][:], "0")
-        x_codes = gather_words(0)
-        for i in range(TILES):
-            multiply(i, 0, h_codes[:, i * P : (i + 1) * P], h_scales[:, i * P : (i + 1) * P], x_codes)
-
-        scatter(TILES - 1, R - LATE, keep.tile([P, LATE], F32, name="weighted_late", tag="grouped0", align_bytes=64))
-        x_codes = gather_words(1)
-        for i in range(TILES):
-            h_codes, h_scales = quantize(h_late[i], "1_%d" % i)
-            multiply(i, 1, h_codes[:], h_scales[:], x_codes)
-        first_cp = keep.tile([P, S], F32, name="first_cp", tag="table_words0")
-        nc.scalar.activation(first_cp[:], copied[0][:], ACT.Copy, scale=cpw_cols[:, 0:1])
-        cp = [first_cp] + copied[1:]
-
-        exps, factors = [], []
-        for i in range(TILES):
-            tag = "grouped1_2" if i == 1 else "minus_max%d" % i
-            minus_max = keep.tile([P, 1], F32, name="minus_max%d" % i, tag=tag, align_bytes=64)
+        def maximum(i, minus_max):
             nc.vector.tensor_reduce(minus_max[:], banks[i][:], mybir.AxisListType.X, ALU.max, negate=True)
-            e = late.tile([P, S], F32, name="exp%d" % i, offset=4 * S * i)
-            total = keep.tile([P, 1], F32, name="total%d" % i)
-            nc.scalar.activation(e[:], banks[i][:], ACT.Exp, bias=minus_max[:], accum_out=total[:])
+            maxima[i] = minus_max
+
+        totals, exps, factors = {}, {}, {}
+
+        def exponentials(i, e):
+            totals[i] = keep.tile([P, 1], F32, name="total%d" % i)
+            nc.scalar.activation(e[:], banks[i][:], ACT.Exp, bias=maxima[i][:], accum_out=totals[i][:])
+            exps[i] = e
+
+        def factor(i):
             inverse = keep.tile([P, 1], F32, name="inverse%d" % i)
-            nc.vector.reciprocal(inverse[:], total[:])
-            factor = keep.tile([P, 1], F32, name="factor%d" % i)
-            nc.scalar.activation(factor[:], inverse[:], ACT.Copy, scale=gen_cols[:, i : i + 1])
-            exps.append(e)
-            factors.append(factor)
-        for i in range(TILES):
-            width = S // 2 if i == TILES - 1 else S
+            nc.vector.reciprocal(inverse[:], totals[i][:])
+            factors[i] = keep.tile([P, 1], F32, name="factor%d" % i)
+            gen_column = weights[:, TILES + i : TILES + i + 1]
+            if i == 0:
+                nc.vector.tensor_mul(factors[i][:], inverse[:], gen_column)
+            else:
+                nc.scalar.activation(factors[i][:], inverse[:], ACT.Copy, scale=gen_column)
+
+        def mix(i):
+            width = S // 2 if i == LAST else S
             for first in range(0, S, width):
                 cols = slice(first, first + width)
                 mixed = keep.tile([P, width], F32, name="mixed%d_%d" % (i, first))
                 nc.vector.scalar_tensor_tensor(mixed[:], exps[i][:, cols], factors[i][:], cp[i][:, cols], ALU.mult, ALU.add)
                 nc.sync.dma_start(out[i * P : (i + 1) * P, cols], mixed[:])
+
+        multiply(0, (0, 1))
+        scatter(LAST, R - LATE, held([P, LATE], "weighted_late", 0, 1))
+        multiply(1, (0, 1))
+        maximum(0, held([P, 1], "minus_max0", 1, 1))
+        multiply(2, (0, 1))
+        maximum(1, held([P, 1], "minus_max1", 2, 1))
+        multiply(LAST, (0,))
+        exponentials(0, held([P, S], "exp0", LAST, 0))
+        maximum(2, keep.tile([P, 1], F32, name="minus_max2"))
+        factor(0)
+        mix(0)
+        multiply(LAST, (1,))
+        exponentials(1, held([P, S], "exp1", LAST, 1, -PIECE_BYTES // 2))
+        exponentials(2, held([P, S], "exp2", LAST, 1, PIECE_BYTES // 2))
+        factor(1)
+        maximum(LAST, keep.tile([P, 1], F32, name="minus_max3"))
+        exponentials(LAST, keep.tile([P, S], F32, name="exp3"))
+        mix(1)
+        factor(2)
+        mix(2)
+        factor(LAST)
+        mix(LAST)

@@ -22,13 +22,10 @@ K_PASS = P * PACK
 PASSES = K // K_PASS
 TILES = V // P
 LAST = TILES - 1
-LATE = R // 2
+RAW = 2
+HALF = V // 2
 ROWS_AT = P - 2 * TILES
 PIECE_BYTES = P * PACK * 4
-
-
-def place(i, o):
-    return (PASSES * i + o + (1 if (i, o) == (LAST, 1) else 0)) * PIECE_BYTES
 
 
 def tile_picked_ycopy_mix_p_kernel(tc, x_words, x_scales, hT, att, cpw, gen, offs, src, out):
@@ -44,18 +41,15 @@ def tile_picked_ycopy_mix_p_kernel(tc, x_words, x_scales, hT, att, cpw, gen, off
         rows = keep.tile([P, P], F32, name="rows")
         identity = keep.tile([P, P], F32, name="identity")
         att_first = keep.tile([P, R], F32, name="att_first")
-        att_middle = early.tile([P, 2, R], F32, name="att_middle", offset=256)
-        att_last = keep.tile([P, R], F32, name="att_last")
+        att_rest = early.tile([P, LAST, R], F32, name="att_rest", offset=256)
         table_scales = keep.tile([P, T // 4], I32, name="table_scales")
         copied = [keep.tile([P, S], F32, name="copied%d" % i) for i in range(TILES)]
         zero = keep.tile([P, 1], F32, name="zero")
         table_words = [keep.tile([P, T], I32, name="table_words%d" % o) for o in range(PASSES)]
-        h_raw = [
-            [late.tile([P, PACK, P], F32, name="h_raw%d_%d" % (i, o), offset=place(i, o)) for o in range(PASSES)]
-            for i in range(TILES)
-        ]
+        h_early = late.tile([P, PACK, V], F32, name="h_early", offset=TILES * PIECE_BYTES)
+        h_late = [late.tile([P, PACK, P], F32, name="h_late%d" % i, offset=i * PIECE_BYTES) for i in range(TILES)]
 
-        nc.vector.memset(table_scales[:], 0)
+        nc.gpsimd.memset(table_scales[:], 0)
         nc.vector.memset(rows[0:ROWS_AT, :], 0.0)
         nc.vector.memset(zero[:], 0.0)
         for i in range(LAST):
@@ -66,20 +60,20 @@ def tile_picked_ycopy_mix_p_kernel(tc, x_words, x_scales, hT, att, cpw, gen, off
         h_view = hT.rearrange("(o p j) t -> o p j t", p=P, j=PACK)
         word_view = x_words.rearrange("o p c r -> o p (c r)").bitcast(I32)
         scale_view = x_scales.bitcast(I32)
-        nc.scalar.dma_start(rows[ROWS_AT : ROWS_AT + TILES, :], cpw.rearrange("(i p) o -> i (p o)", p=P))
-        nc.scalar.dma_start(rows[ROWS_AT + TILES : P, :], gen.rearrange("(i p) o -> i (p o)", p=P))
         nc.sync.dma_start(src_list[:], src)
         nc.sync.dma_start(att_first[:], att_view[:, 0, :])
-        nc.sync.dma_start(att_middle[:], att_view[:, 1:LAST, :])
-        nc.sync.dma_start(att_last[:], att_view[:, LAST, :])
-        nc.sync.dma_start(table_words[0][:], word_view[0])
-        for q in range(4):
+        for q in (2, 3, 0, 1):
             nc.sync.dma_start(table_scales[32 * q : 32 * q + 4 * PASSES, :], scale_view[:, 4 * q : 4 * q + 4, :])
+        nc.sync.dma_start(att_rest[:], att_view[:, 1:, :])
+        nc.sync.dma_start(rows[ROWS_AT : ROWS_AT + TILES, :], cpw.rearrange("(i p) o -> i (p o)", p=P))
+        nc.sync.dma_start(rows[ROWS_AT + TILES : P, :], gen.rearrange("(i p) o -> i (p o)", p=P))
+        nc.sync.dma_start(h_early[:], h_view[0])
         nc.sync.dma_start(offs_list[:], offs)
-        nc.sync.dma_start(table_words[1][:], word_view[1])
+        nc.sync.dma_start(table_words[0][:], word_view[0])
         for i in range(TILES):
-            for o in range(PASSES):
-                nc.sync.dma_start(h_raw[i][o][:], h_view[o][:, :, i * P : (i + 1) * P])
+            nc.sync.dma_start(h_late[i][:], h_view[1][:, :, i * P : (i + 1) * P])
+            if i == 0:
+                nc.sync.dma_start(table_words[1][:], word_view[1])
 
         nc.scalar.activation(copied[LAST][:], zero[:].to_broadcast([P, S]), ACT.Copy)
         turned = psum.tile([P, P], F32, name="turned")
@@ -89,55 +83,74 @@ def tile_picked_ycopy_mix_p_kernel(tc, x_words, x_scales, hT, att, cpw, gen, off
 
         nc.vector.tensor_copy(copied[0][:].indirect(src_list[:]), att_first[:])
 
-        def scatter(i, first, weighted):
-            count = weighted.shape[1]
-            values = (att_last if i == LAST else att_middle[:, i - 1, :])[:, first : first + count]
-            nc.scalar.activation(weighted[:], values, ACT.Copy, scale=weights[:, i : i + 1])
-            places = src_list[:, first // 16 : (first + count) // 16]
-            nc.vector.tensor_copy(copied[i][:].indirect(places), weighted[:])
-
-        scatter(1, 0, keep.tile([P, R], F32, name="weighted1", tag="weighted1"))
-        scatter(2, 0, keep.tile([P, R], F32, name="weighted2"))
-        scatter(LAST, 0, keep.tile([P, R - LATE], F32, name="weighted3"))
-        first_cp = keep.tile([P, S], F32, name="first_cp", tag="weighted1")
-        nc.scalar.activation(first_cp[:], copied[0][:], ACT.Copy, scale=weights[:, 0:1])
-        cp = [first_cp] + copied[1:]
+        nc.vector.tensor_copy(copied[1][:].indirect(src_list[:]), att_rest[:, 0, :])
+        for i in range(RAW, TILES):
+            weighted = keep.tile([P, R], F32, name="weighted%d" % i)
+            nc.scalar.activation(weighted[:], att_rest[:, i - 1, :], ACT.Copy, scale=weights[:, i : i + 1])
+            nc.vector.tensor_copy(copied[i][:].indirect(src_list[:]), weighted[:])
 
         x_planes = early.tile([P, S], U8, name="x_planes", align_bytes=64, offset=0)
         nc.vector.tensor_copy(x_planes[:], table_scales[:].bitcast(U8).indirect(offs_list[:]))
-        x_codes = []
-        for o in range(PASSES):
-            codes = early.tile([P, S], U32, name="x_codes%d" % o, align_bytes=64, offset=S + 4 * S * o)
-            nc.vector.tensor_copy(codes[:], table_words[o][:].bitcast(U32).indirect(offs_list[:]))
-            x_codes.append(codes)
-
         banks = [psum.tile([P, S], F32, name="logits%d" % i) for i in range(TILES)]
 
-        def multiply(i, passes):
-            name = "%d_%d" % (i, passes[0])
-            width = P * len(passes)
-            grouped = keep.tile([P, width, PACK], BF16, name="grouped" + name, align_bytes=64)
-            for n, o in enumerate(passes):
-                nc.scalar.copy(
-                    grouped[:, n * P : (n + 1) * P, :].rearrange("p (c i) j -> p c j i", i=4),
-                    h_raw[i][o][:].rearrange("p j (c i) -> p c j i", i=4),
-                )
-            codes = keep.tile([P, width], U32, name="h_codes" + name, align_bytes=64)
-            scales = keep.tile([P, width], U8, name="h_scales" + name, align_bytes=64)
-            nc.vector.quantize_mx(out=codes[:].bitcast(FP8X4), scales=scales[:], in_=grouped[:].rearrange("p t j -> p (t j)"))
-            for n, o in enumerate(passes):
-                nc.tensor.matmul_mx(
-                    out=banks[i][:],
-                    lhsT=codes[:, n * P : (n + 1) * P].bitcast(FP8X4),
-                    lhsT_scale=scales[:, n * P : (n + 1) * P],
-                    rhs=x_codes[o][:].bitcast(FP8X4),
-                    rhs_scale=x_planes[4 * o : P, :],
-                    start=(o == 0),
-                    stop=(o == PASSES - 1),
-                )
+        def gather_words(o):
+            codes = early.tile([P, S], U32, name="x_codes%d" % o, align_bytes=64, offset=S + 12 * S * o)
+            nc.vector.tensor_copy(codes[:], table_words[o][:].bitcast(U32).indirect(offs_list[:]))
+            return codes
 
-        def held(shape, name, i, o, first=0):
-            return late.tile(shape, F32, name=name, offset=place(i, o) + first)
+        def interleave(raw, grouped):
+            nc.scalar.copy(
+                grouped.rearrange("p (c i) j -> p c j i", i=4),
+                raw.rearrange("p j (c i) -> p c j i", i=4),
+            )
+            return grouped
+
+        def quantize(grouped, name, codes):
+            width = grouped.shape[1]
+            scales = keep.tile([P, width], U8, name="h_scales" + name, align_bytes=64)
+            nc.vector.quantize_mx(out=codes[:].bitcast(FP8X4), scales=scales[:], in_=grouped.rearrange("p t j -> p (t j)"))
+            return codes, scales
+
+        def multiply(i, o, h_codes, h_scales, x_codes):
+            nc.tensor.matmul_mx(
+                out=banks[i][:],
+                lhsT=h_codes.bitcast(FP8X4),
+                lhsT_scale=h_scales,
+                rhs=x_codes[:].bitcast(FP8X4),
+                rhs_scale=x_planes[4 * o : P, :],
+                start=(o == 0),
+                stop=(o == PASSES - 1),
+            )
+
+        grouped_early = early.tile([P, V, PACK], BF16, name="grouped_early", align_bytes=64, offset=5 * S)
+        halves = [interleave(h_early[:, :, u * HALF : (u + 1) * HALF], grouped_early[:, u * HALF : (u + 1) * HALF, :]) for u in range(2)]
+        x_codes = [gather_words(0)]
+
+        def first_pass(i, half):
+            cols = slice((i % 2) * P, (i % 2 + 1) * P)
+            multiply(i, 0, half[0][:, cols], half[1][:, cols], x_codes[0])
+
+        def late_codes(i):
+            grouped = keep.tile([P, P, PACK], BF16, name="grouped%d" % i, align_bytes=64)
+            return quantize(interleave(h_late[i][:], grouped[:]), "%d" % i, keep.tile([P, P], U32, name="h_codes%d" % i, align_bytes=64))
+
+        half = quantize(halves[0], "_half0", keep.tile([P, HALF], U32, name="h_codes_half0", align_bytes=64))
+        first_pass(0, half)
+        first_pass(1, half)
+        cp = list(copied)
+        for i in range(RAW):
+            cp[i] = late.tile([P, S], F32, name="cp%d" % i, offset=(TILES + i) * PIECE_BYTES)
+            nc.scalar.activation(cp[i][:], copied[i][:], ACT.Copy, scale=weights[:, i : i + 1])
+        h_codes, h_scales = late_codes(0)
+        x_codes.append(gather_words(1))
+        multiply(0, 1, h_codes[:], h_scales[:], x_codes[1])
+
+        def second_pass(i):
+            h_codes, h_scales = late_codes(i)
+            multiply(i, 1, h_codes[:], h_scales[:], x_codes[1])
+
+        def held(shape, name, i):
+            return late.tile(shape, F32, name=name, offset=i * PIECE_BYTES)
 
         maxima = {}
 
@@ -156,11 +169,7 @@ def tile_picked_ycopy_mix_p_kernel(tc, x_words, x_scales, hT, att, cpw, gen, off
             inverse = keep.tile([P, 1], F32, name="inverse%d" % i)
             nc.vector.reciprocal(inverse[:], totals[i][:])
             factors[i] = keep.tile([P, 1], F32, name="factor%d" % i)
-            gen_column = weights[:, TILES + i : TILES + i + 1]
-            if i == 0:
-                nc.vector.tensor_mul(factors[i][:], inverse[:], gen_column)
-            else:
-                nc.scalar.activation(factors[i][:], inverse[:], ACT.Copy, scale=gen_column)
+            nc.scalar.activation(factors[i][:], inverse[:], ACT.Copy, scale=weights[:, TILES + i : TILES + i + 1])
 
         def mix(i):
             width = S // 2 if i == LAST else S
@@ -170,25 +179,21 @@ def tile_picked_ycopy_mix_p_kernel(tc, x_words, x_scales, hT, att, cpw, gen, off
                 nc.vector.scalar_tensor_tensor(mixed[:], exps[i][:, cols], factors[i][:], cp[i][:, cols], ALU.mult, ALU.add)
                 nc.sync.dma_start(out[i * P : (i + 1) * P, cols], mixed[:])
 
-        multiply(0, (0, 1))
-        scatter(LAST, R - LATE, held([P, LATE], "weighted_late", 0, 1))
-        multiply(1, (0, 1))
-        maximum(0, held([P, 1], "minus_max0", 1, 1))
-        multiply(2, (0, 1))
-        maximum(1, held([P, 1], "minus_max1", 2, 1))
-        multiply(LAST, (0,))
-        exponentials(0, held([P, S], "exp0", LAST, 0))
-        maximum(2, keep.tile([P, 1], F32, name="minus_max2"))
-        factor(0)
-        mix(0)
-        multiply(LAST, (1,))
-        exponentials(1, held([P, S], "exp1", LAST, 1, -PIECE_BYTES // 2))
-        exponentials(2, held([P, S], "exp2", LAST, 1, PIECE_BYTES // 2))
-        factor(1)
-        maximum(LAST, keep.tile([P, 1], F32, name="minus_max3"))
-        exponentials(LAST, keep.tile([P, S], F32, name="exp3"))
-        mix(1)
-        factor(2)
-        mix(2)
-        factor(LAST)
-        mix(LAST)
+        second_pass(1)
+        half = quantize(halves[1], "_half1", late.tile([P, HALF], U32, name="h_codes_half1", align_bytes=64, offset=PIECE_BYTES + 64))
+        first_pass(2, half)
+        first_pass(LAST, half)
+        maximum(0, held([P, 1], "minus_max0", 1))
+        second_pass(2)
+        maximum(1, held([P, 1], "minus_max1", 2))
+        second_pass(LAST)
+        exponentials(0, held([P, S], "exp0", LAST))
+        exponentials(1, keep.tile([P, S], F32, name="exp1"))
+        for i in range(2, TILES):
+            maximum(i, keep.tile([P, 1], F32, name="minus_max%d" % i))
+            exponentials(i, keep.tile([P, S], F32, name="exp%d" % i))
+            factor(i - 2)
+        for i in range(TILES):
+            mix(i)
+            if i + 2 < TILES:
+                factor(i + 2)

@@ -50,10 +50,9 @@ def tile_picked_ycopy_mix_p_kernel(tc, x_words, x_scales, hT, att, cpw, gen, off
         h_late = [late.tile([P, PACK, P], F32, name="h_late%d" % i, offset=i * PIECE_BYTES) for i in range(TILES)]
 
         nc.gpsimd.memset(table_scales[:], 0)
-        nc.vector.memset(rows[0:ROWS_AT, :], 0.0)
         nc.vector.memset(zero[:], 0.0)
-        for i in range(LAST):
-            nc.vector.memset(copied[i][:], 0.0)
+        nc.vector.memset(rows[0:ROWS_AT, :], 0.0)
+        nc.vector.memset(copied[0][:], 0.0)
         make_identity(nc, identity[:])
 
         att_view = att.rearrange("(i p) r -> p i r", p=P)
@@ -62,9 +61,9 @@ def tile_picked_ycopy_mix_p_kernel(tc, x_words, x_scales, hT, att, cpw, gen, off
         scale_view = x_scales.bitcast(I32)
         nc.sync.dma_start(src_list[:], src)
         nc.sync.dma_start(att_first[:], att_view[:, 0, :])
+        nc.sync.dma_start(att_rest[:], att_view[:, 1:, :])
         for q in (2, 3, 0, 1):
             nc.sync.dma_start(table_scales[32 * q : 32 * q + 4 * PASSES, :], scale_view[:, 4 * q : 4 * q + 4, :])
-        nc.sync.dma_start(att_rest[:], att_view[:, 1:, :])
         nc.sync.dma_start(rows[ROWS_AT : ROWS_AT + TILES, :], cpw.rearrange("(i p) o -> i (p o)", p=P))
         nc.sync.dma_start(rows[ROWS_AT + TILES : P, :], gen.rearrange("(i p) o -> i (p o)", p=P))
         nc.sync.dma_start(h_early[:], h_view[0])
@@ -75,7 +74,8 @@ def tile_picked_ycopy_mix_p_kernel(tc, x_words, x_scales, hT, att, cpw, gen, off
             if i == 0:
                 nc.sync.dma_start(table_words[1][:], word_view[1])
 
-        nc.scalar.activation(copied[LAST][:], zero[:].to_broadcast([P, S]), ACT.Copy)
+        for i in range(1, TILES):
+            nc.scalar.activation(copied[i][:], zero[:].to_broadcast([P, S]), ACT.Copy)
         turned = psum.tile([P, P], F32, name="turned")
         nc.tensor.transpose(turned[:], rows[:], identity[:])
         weights = keep.tile([P, 2 * TILES], F32, name="weights")

@@ -58,17 +58,23 @@ def tile_picked_ycopy_mix_p_kernel(tc, x_words, x_scales, hT, att, cpw, gen, off
         att_view = att.rearrange("(i p) r -> p i r", p=P)
         h_view = hT.rearrange("(o p j) t -> o p j t", p=P, j=PACK)
         word_view = x_words.rearrange("o p c r -> o p (c r)").bitcast(I32)
-        scale_view = x_scales.bitcast(I32)
-        nc.sync.dma_start(src_list[:], src)
+        scale_view = x_scales.bitcast(I32).rearrange("o (q j) n -> o j q n", j=4)
+
+        def load_scale_rows(rows_j):
+            for j in rows_j:
+                for o in range(PASSES):
+                    nc.sync.dma_start(table_scales[4 * o + j : P : 32, :], scale_view[o, j])
+
         nc.sync.dma_start(att_first[:], att_view[:, 0, :])
+        nc.sync.dma_start(src_list[:], src)
         nc.sync.dma_start(att_rest[:], att_view[:, 1:, :])
-        for q in (2, 3, 0, 1):
-            nc.sync.dma_start(table_scales[32 * q : 32 * q + 4 * PASSES, :], scale_view[:, 4 * q : 4 * q + 4, :])
+        load_scale_rows((0, 1))
         nc.sync.dma_start(rows[ROWS_AT : ROWS_AT + TILES, :], cpw.rearrange("(i p) o -> i (p o)", p=P))
         nc.sync.dma_start(rows[ROWS_AT + TILES : P, :], gen.rearrange("(i p) o -> i (p o)", p=P))
         nc.sync.dma_start(h_early[:], h_view[0])
-        nc.sync.dma_start(offs_list[:], offs)
+        load_scale_rows((2, 3))
         nc.sync.dma_start(table_words[0][:], word_view[0])
+        nc.sync.dma_start(offs_list[:], offs)
         for i in range(TILES):
             nc.sync.dma_start(h_late[i][:], h_view[1][:, :, i * P : (i + 1) * P])
             if i == 0:

@@ -1,7 +1,6 @@
 from contextlib import ExitStack
 
 import concourse.mybir as mybir
-from concourse.masks import make_identity
 
 K, T, S, V, R = 1024, 2048, 512, 512, 256
 FLOPS = 2 * K * V * S
@@ -22,9 +21,7 @@ K_PASS = P * PACK
 PASSES = K // K_PASS
 TILES = V // P
 LAST = TILES - 1
-RAW = 2
 HALF = V // 2
-ROWS_AT = P - 2 * TILES
 PIECE_BYTES = P * PACK * 4
 
 
@@ -38,74 +35,79 @@ def tile_picked_ycopy_mix_p_kernel(tc, x_words, x_scales, hT, att, cpw, gen, off
 
         src_list = keep.tile([P, R // 16], U16, name="src_list")
         offs_list = keep.tile([P, S // 16], U16, name="offs_list")
-        rows = keep.tile([P, P], F32, name="rows")
-        identity = keep.tile([P, P], F32, name="identity")
-        att_first = keep.tile([P, R], F32, name="att_first")
-        att_rest = early.tile([P, LAST, R], F32, name="att_rest", offset=256)
-        table_scales = keep.tile([P, T // 4], I32, name="table_scales")
-        copied = [keep.tile([P, S], F32, name="copied%d" % i) for i in range(TILES)]
+        copy_weight = keep.tile([P, TILES, 8], F32, name="copy_weight")
+        att_all = early.tile([P, TILES, R], F32, name="att_all", align_bytes=64, offset=8 * S)
+        table_scales = early.tile([P, T // 4], I32, name="table_scales", align_bytes=64, offset=2 * S)
+        cp = [keep.tile([P, S], F32, name="cp%d" % i) for i in range(TILES)]
         zero = keep.tile([P, 1], F32, name="zero")
-        table_words = [keep.tile([P, T], I32, name="table_words%d" % o) for o in range(PASSES)]
-        h_early = late.tile([P, PACK, V], F32, name="h_early", offset=TILES * PIECE_BYTES)
-        h_late = [late.tile([P, PACK, P], F32, name="h_late%d" % i, offset=i * PIECE_BYTES) for i in range(TILES)]
+        table_words = [late.tile([P, T], I32, name="table_words0", offset=PIECE_BYTES), None]
+        h_early = keep.tile([P, PACK, V], F32, name="h_early")
+        planes = [keep.tile([P, S], U8, name="plane0", align_bytes=64), None]
 
         nc.gpsimd.memset(table_scales[:], 0)
         nc.vector.memset(zero[:], 0.0)
-        nc.vector.memset(rows[0:ROWS_AT, :], 0.0)
-        nc.vector.memset(copied[0][:], 0.0)
-        make_identity(nc, identity[:])
+        nc.vector.memset(planes[0][:].bitcast(I32), 0)
+        for i in range(2):
+            nc.vector.memset(cp[i][:], 0.0)
 
         att_view = att.rearrange("(i p) r -> p i r", p=P)
         h_view = hT.rearrange("(o p j) t -> o p j t", p=P, j=PACK)
         word_view = x_words.rearrange("o p c r -> o p (c r)").bitcast(I32)
-        scale_view = x_scales.bitcast(I32).rearrange("o (q j) n -> o j q n", j=4)
+        scale_view = x_scales.bitcast(I32).rearrange("o r n -> (o r) n")
 
-        def load_scale_rows(rows_j):
-            for j in rows_j:
-                for o in range(PASSES):
-                    nc.sync.dma_start(table_scales[4 * o + j : P : 32, :], scale_view[o, j])
+        def load_column(tile, column):
+            with nc.allow_non_contiguous_dma(reason="one value a position"):
+                nc.sync.dma_start(tile[:, :, 0:1], column.rearrange("(i p) o -> p i o", p=P))
 
-        nc.sync.dma_start(att_first[:], att_view[:, 0, :])
+        nc.sync.dma_start(att_all[:], att_view)
+        load_column(copy_weight, cpw)
         nc.sync.dma_start(src_list[:], src)
-        nc.sync.dma_start(att_rest[:], att_view[:, 1:, :])
-        load_scale_rows((0, 1))
-        nc.sync.dma_start(rows[ROWS_AT : ROWS_AT + TILES, :], cpw.rearrange("(i p) o -> i (p o)", p=P))
-        nc.sync.dma_start(rows[ROWS_AT + TILES : P, :], gen.rearrange("(i p) o -> i (p o)", p=P))
-        nc.sync.dma_start(h_early[:], h_view[0])
-        load_scale_rows((2, 3))
-        nc.sync.dma_start(table_words[0][:], word_view[0])
         nc.sync.dma_start(offs_list[:], offs)
-        for i in range(TILES):
-            nc.sync.dma_start(h_late[i][:], h_view[1][:, :, i * P : (i + 1) * P])
-            if i == 0:
-                nc.sync.dma_start(table_words[1][:], word_view[1])
+        nc.sync.dma_start(table_scales[0:P:4, :], scale_view)
+        nc.sync.dma_start(table_words[0][:], word_view[0])
+        nc.sync.dma_start(h_early[:], h_view[0])
 
+        for i in range(2, TILES):
+            nc.scalar.activation(cp[i][:], zero[:].to_broadcast([P, S]), ACT.Copy)
+
+        weighted = {}
+
+        def weigh(i, tile):
+            weighted[i] = tile
+            nc.vector.tensor_scalar(tile[:], att_all[:, i, :], copy_weight[:, i, 0:1], None, ALU.mult)
+
+        for i in (1, 2):
+            weigh(i, keep.tile([P, R], F32, name="weighted%d" % i))
+        picked = keep.tile([P, S], U8, name="picked", align_bytes=64)
+        nc.vector.tensor_copy(picked[:], table_scales[:].bitcast(U8).indirect(offs_list[:]))
+
+        def move_scale_rows(o):
+            for j in range(4):
+                nc.sync.dma_start(planes[o][j:P:32, :].bitcast(I32), picked[64 * o + 4 * j : 64 * (o + 1) : 16, :].bitcast(I32))
+
+        move_scale_rows(0)
+        for n, i in enumerate((0, 3)):
+            weigh(i, early.tile([P, R], F32, name="weighted%d" % i, offset=4 * R * (n + 1)))
+        table_words[1] = early.tile([P, T], I32, name="table_words1", align_bytes=64, offset=12 * S)
+        nc.sync.dma_start(table_words[1][:], word_view[1])
+        h_late = [early.tile([P, PACK, P], F32, name="h_late0", align_bytes=64, offset=8 * S)]
+        nc.sync.dma_start(h_late[0][:], h_view[1][:, :, 0:P])
+        nc.vector.tensor_copy(cp[0][:].indirect(src_list[:]), weighted[0][:])
         for i in range(1, TILES):
-            nc.scalar.activation(copied[i][:], zero[:].to_broadcast([P, S]), ACT.Copy)
-        turned = psum.tile([P, P], F32, name="turned")
-        nc.tensor.transpose(turned[:], rows[:], identity[:])
-        weights = keep.tile([P, 2 * TILES], F32, name="weights")
-        nc.scalar.copy(weights[:], turned[:, ROWS_AT:P])
+            nc.scalar.activation(cp[i][:].indirect(src_list[:]), weighted[i][:], ACT.Copy)
+        planes[1] = early.tile([P, S], U8, name="plane1", align_bytes=64, offset=5 * R)
+        nc.gpsimd.memset(planes[1][:].bitcast(I32), 0)
+        move_scale_rows(1)
 
-        nc.vector.tensor_copy(copied[0][:].indirect(src_list[:]), att_first[:])
-
-        nc.vector.tensor_copy(copied[1][:].indirect(src_list[:]), att_rest[:, 0, :])
-        for i in range(RAW, TILES):
-            weighted = keep.tile([P, R], F32, name="weighted%d" % i)
-            nc.scalar.activation(weighted[:], att_rest[:, i - 1, :], ACT.Copy, scale=weights[:, i : i + 1])
-            nc.vector.tensor_copy(copied[i][:].indirect(src_list[:]), weighted[:])
-
-        x_planes = early.tile([P, S], U8, name="x_planes", align_bytes=64, offset=0)
-        nc.vector.tensor_copy(x_planes[:], table_scales[:].bitcast(U8).indirect(offs_list[:]))
         banks = [psum.tile([P, S], F32, name="logits%d" % i) for i in range(TILES)]
 
         def gather_words(o):
-            codes = early.tile([P, S], U32, name="x_codes%d" % o, align_bytes=64, offset=S + 12 * S * o)
+            codes = keep.tile([P, S], U32, name="x_codes%d" % o, align_bytes=64)
             nc.vector.tensor_copy(codes[:], table_words[o][:].bitcast(U32).indirect(offs_list[:]))
             return codes
 
-        def interleave(raw, grouped):
-            nc.scalar.copy(
+        def interleave(raw, grouped, copy=nc.scalar.copy):
+            copy(
                 grouped.rearrange("p (c i) j -> p c j i", i=4),
                 raw.rearrange("p j (c i) -> p c j i", i=4),
             )
@@ -123,14 +125,22 @@ def tile_picked_ycopy_mix_p_kernel(tc, x_words, x_scales, hT, att, cpw, gen, off
                 lhsT=h_codes.bitcast(FP8X4),
                 lhsT_scale=h_scales,
                 rhs=x_codes[:].bitcast(FP8X4),
-                rhs_scale=x_planes[4 * o : P, :],
+                rhs_scale=planes[o][:],
                 start=(o == 0),
                 stop=(o == PASSES - 1),
             )
 
-        grouped_early = early.tile([P, V, PACK], BF16, name="grouped_early", align_bytes=64, offset=5 * S)
-        halves = [interleave(h_early[:, :, u * HALF : (u + 1) * HALF], grouped_early[:, u * HALF : (u + 1) * HALF, :]) for u in range(2)]
+        grouped_early = [keep.tile([P, HALF, PACK], BF16, name="grouped_early%d" % u, align_bytes=64) for u in range(2)]
         x_codes = [gather_words(0)]
+        for i in range(1, TILES):
+            h_late.append(late.tile([P, PACK, P], F32, name="h_late%d" % i, offset=i * PIECE_BYTES))
+            nc.sync.dma_start(h_late[i][:], h_view[1][:, :, i * P : (i + 1) * P])
+        gen_weight = late.tile([P, TILES, 8], F32, name="gen_weight", offset=TILES * PIECE_BYTES)
+        load_column(gen_weight, gen)
+        halves = [
+            interleave(h_early[:, :, 0:HALF], grouped_early[0][:], nc.vector.tensor_copy),
+            interleave(h_early[:, :, HALF:V], grouped_early[1][:]),
+        ]
 
         def first_pass(i, half):
             cols = slice((i % 2) * P, (i % 2 + 1) * P)
@@ -143,12 +153,11 @@ def tile_picked_ycopy_mix_p_kernel(tc, x_words, x_scales, hT, att, cpw, gen, off
         half = quantize(halves[0], "_half0", keep.tile([P, HALF], U32, name="h_codes_half0", align_bytes=64))
         first_pass(0, half)
         first_pass(1, half)
-        cp = list(copied)
-        for i in range(RAW):
-            cp[i] = late.tile([P, S], F32, name="cp%d" % i, offset=(TILES + i) * PIECE_BYTES)
-            nc.scalar.activation(cp[i][:], copied[i][:], ACT.Copy, scale=weights[:, i : i + 1])
-        h_codes, h_scales = late_codes(0)
+        half = quantize(halves[1], "_half1", keep.tile([P, HALF], U32, name="h_codes_half1", align_bytes=64))
+        first_pass(2, half)
+        first_pass(LAST, half)
         x_codes.append(gather_words(1))
+        h_codes, h_scales = late_codes(0)
         multiply(0, 1, h_codes[:], h_scales[:], x_codes[1])
 
         def second_pass(i):
@@ -175,7 +184,7 @@ def tile_picked_ycopy_mix_p_kernel(tc, x_words, x_scales, hT, att, cpw, gen, off
             inverse = keep.tile([P, 1], F32, name="inverse%d" % i)
             nc.vector.reciprocal(inverse[:], totals[i][:])
             factors[i] = keep.tile([P, 1], F32, name="factor%d" % i)
-            nc.scalar.activation(factors[i][:], inverse[:], ACT.Copy, scale=weights[:, TILES + i : TILES + i + 1])
+            nc.scalar.activation(factors[i][:], inverse[:], ACT.Copy, scale=gen_weight[:, i, 0:1])
 
         def mix(i):
             width = S // 2 if i == LAST else S
@@ -186,9 +195,6 @@ def tile_picked_ycopy_mix_p_kernel(tc, x_words, x_scales, hT, att, cpw, gen, off
                 nc.sync.dma_start(out[i * P : (i + 1) * P, cols], mixed[:])
 
         second_pass(1)
-        half = quantize(halves[1], "_half1", late.tile([P, HALF], U32, name="h_codes_half1", align_bytes=64, offset=PIECE_BYTES + 64))
-        first_pass(2, half)
-        first_pass(LAST, half)
         maximum(0, held([P, 1], "minus_max0", 1))
         second_pass(2)
         maximum(1, held([P, 1], "minus_max1", 2))

@@ -89,9 +89,9 @@ def tile_picked_ycopy_mix_p_kernel(tc, x_words, x_scales, hT, att, cpw, gen, off
         for n, i in enumerate((0, 3)):
             weigh(i, early.tile([P, R], F32, name="weighted%d" % i, offset=4 * R * (n + 1)))
         table_words[1] = early.tile([P, T], I32, name="table_words1", align_bytes=64, offset=12 * S)
-        nc.sync.dma_start(table_words[1][:], word_view[1])
         h_late = [early.tile([P, PACK, P], F32, name="h_late0", align_bytes=64, offset=8 * S)]
         nc.sync.dma_start(h_late[0][:], h_view[1][:, :, 0:P])
+        nc.sync.dma_start(table_words[1][:], word_view[1])
         nc.vector.tensor_copy(cp[0][:].indirect(src_list[:]), weighted[0][:])
         for i in range(1, TILES):
             nc.scalar.activation(cp[i][:].indirect(src_list[:]), weighted[i][:], ACT.Copy)
@@ -156,9 +156,21 @@ def tile_picked_ycopy_mix_p_kernel(tc, x_words, x_scales, hT, att, cpw, gen, off
         half = quantize(halves[1], "_half1", keep.tile([P, HALF], U32, name="h_codes_half1", align_bytes=64))
         first_pass(2, half)
         first_pass(LAST, half)
-        x_codes.append(gather_words(1))
         h_codes, h_scales = late_codes(0)
-        multiply(0, 1, h_codes[:], h_scales[:], x_codes[1])
+        x_codes.append(keep.tile([P, S], U32, name="x_codes1", align_bytes=64))
+        for u in range(2):
+            cols = slice(u * S // 2, (u + 1) * S // 2)
+            entries = offs_list[:, u * S // 32 : (u + 1) * S // 32]
+            nc.vector.tensor_copy(x_codes[1][:, cols], table_words[1][:].bitcast(U32).indirect(entries))
+            nc.tensor.matmul_mx(
+                out=banks[0][:, cols],
+                lhsT=h_codes[:].bitcast(FP8X4),
+                lhsT_scale=h_scales[:],
+                rhs=x_codes[1][:, cols].bitcast(FP8X4),
+                rhs_scale=planes[1][:, cols],
+                start=False,
+                stop=(u == 1),
+            )
 
         def second_pass(i):
             h_codes, h_scales = late_codes(i)

from contextlib import ExitStack

import concourse.mybir as mybir

K, T, S, V, R = 1024, 2048, 512, 512, 256
FLOPS = 2 * K * V * S

F32 = mybir.dt.float32
BF16 = mybir.dt.bfloat16
I32 = mybir.dt.int32
U32 = mybir.dt.uint32
U16 = mybir.dt.uint16
U8 = mybir.dt.uint8
FP8X4 = mybir.dt.float8_e4m3fn_x4
ACT = mybir.ActivationFunctionType
ALU = mybir.AluOpType

P = 128
PACK = 4
K_PASS = P * PACK
PASSES = K // K_PASS
TILES = V // P
LAST = TILES - 1
HALF = V // 2
PIECE_BYTES = P * PACK * 4


def tile_picked_ycopy_mix_p_kernel(tc, x_words, x_scales, hT, att, cpw, gen, offs, src, out):
    nc = tc.nc
    with ExitStack() as ctx:
        keep = ctx.enter_context(tc.tile_pool(name="keep", bufs=1))
        late = ctx.enter_context(tc.tile_pool(name="late", bufs=1))
        early = ctx.enter_context(tc.tile_pool(name="early", bufs=1))
        psum = ctx.enter_context(tc.psum_pool(name="psum", bufs=1))

        src_list = keep.tile([P, R // 16], U16, name="src_list")
        offs_list = keep.tile([P, S // 16], U16, name="offs_list")
        copy_weight = keep.tile([P, TILES, 8], F32, name="copy_weight")
        att_all = early.tile([P, TILES, R], F32, name="att_all", align_bytes=64, offset=8 * S)
        table_scales = early.tile([P, T // 4], I32, name="table_scales", align_bytes=64, offset=2 * S)
        cp = [keep.tile([P, S], F32, name="cp%d" % i) for i in range(TILES)]
        zero = keep.tile([P, 1], F32, name="zero")
        table_words = [late.tile([P, T], I32, name="table_words0", offset=PIECE_BYTES), None]
        h_early = keep.tile([P, PACK, V], F32, name="h_early")
        planes = [keep.tile([P, S], U8, name="plane0", align_bytes=64), None]

        nc.gpsimd.memset(table_scales[:], 0)
        nc.vector.memset(zero[:], 0.0)
        nc.vector.memset(planes[0][:].bitcast(I32), 0)
        for i in range(2):
            nc.vector.memset(cp[i][:], 0.0)

        att_view = att.rearrange("(i p) r -> p i r", p=P)
        h_view = hT.rearrange("(o p j) t -> o p j t", p=P, j=PACK)
        word_view = x_words.rearrange("o p c r -> o p (c r)").bitcast(I32)
        scale_view = x_scales.bitcast(I32).rearrange("o r n -> (o r) n")

        def load_column(tile, column):
            with nc.allow_non_contiguous_dma(reason="one value a position"):
                nc.sync.dma_start(tile[:, :, 0:1], column.rearrange("(i p) o -> p i o", p=P))

        nc.sync.dma_start(att_all[:], att_view)
        load_column(copy_weight, cpw)
        nc.sync.dma_start(src_list[:], src)
        nc.sync.dma_start(offs_list[:], offs)
        nc.sync.dma_start(table_scales[0:P:4, :], scale_view)
        nc.sync.dma_start(table_words[0][:], word_view[0])
        nc.sync.dma_start(h_early[:], h_view[0])

        for i in range(2, TILES):
            nc.scalar.activation(cp[i][:], zero[:].to_broadcast([P, S]), ACT.Copy)

        weighted = {}

        def weigh(i, tile):
            weighted[i] = tile
            nc.vector.tensor_scalar(tile[:], att_all[:, i, :], copy_weight[:, i, 0:1], None, ALU.mult)

        for i in (1, 2):
            weigh(i, keep.tile([P, R], F32, name="weighted%d" % i))
        picked = keep.tile([P, S], U8, name="picked", align_bytes=64)
        nc.vector.tensor_copy(picked[:], table_scales[:].bitcast(U8).indirect(offs_list[:]))

        def move_scale_rows(o):
            for j in range(4):
                nc.sync.dma_start(planes[o][j:P:32, :].bitcast(I32), picked[64 * o + 4 * j : 64 * (o + 1) : 16, :].bitcast(I32))

        move_scale_rows(0)
        for n, i in enumerate((0, 3)):
            weigh(i, early.tile([P, R], F32, name="weighted%d" % i, offset=4 * R * (n + 1)))
        table_words[1] = early.tile([P, T], I32, name="table_words1", align_bytes=64, offset=12 * S)
        h_late = [early.tile([P, PACK, P], F32, name="h_late0", align_bytes=64, offset=8 * S)]
        nc.sync.dma_start(h_late[0][:], h_view[1][:, :, 0:P])
        nc.sync.dma_start(table_words[1][:], word_view[1])
        nc.vector.tensor_copy(cp[0][:].indirect(src_list[:]), weighted[0][:])
        for i in range(1, TILES):
            nc.scalar.activation(cp[i][:].indirect(src_list[:]), weighted[i][:], ACT.Copy)
        planes[1] = early.tile([P, S], U8, name="plane1", align_bytes=64, offset=5 * R)
        nc.gpsimd.memset(planes[1][:].bitcast(I32), 0)
        move_scale_rows(1)

        banks = [psum.tile([P, S], F32, name="logits%d" % i) for i in range(TILES)]

        def gather_words(o):
            codes = keep.tile([P, S], U32, name="x_codes%d" % o, align_bytes=64)
            nc.vector.tensor_copy(codes[:], table_words[o][:].bitcast(U32).indirect(offs_list[:]))
            return codes

        def interleave(raw, grouped, copy=nc.scalar.copy):
            copy(
                grouped.rearrange("p (c i) j -> p c j i", i=4),
                raw.rearrange("p j (c i) -> p c j i", i=4),
            )
            return grouped

        def quantize(grouped, name, codes):
            width = grouped.shape[1]
            scales = keep.tile([P, width], U8, name="h_scales" + name, align_bytes=64)
            nc.vector.quantize_mx(out=codes[:].bitcast(FP8X4), scales=scales[:], in_=grouped.rearrange("p t j -> p (t j)"))
            return codes, scales

        def multiply(i, o, h_codes, h_scales, x_codes):
            nc.tensor.matmul_mx(
                out=banks[i][:],
                lhsT=h_codes.bitcast(FP8X4),
                lhsT_scale=h_scales,
                rhs=x_codes[:].bitcast(FP8X4),
                rhs_scale=planes[o][:],
                start=(o == 0),
                stop=(o == PASSES - 1),
            )

        grouped_early = [keep.tile([P, HALF, PACK], BF16, name="grouped_early%d" % u, align_bytes=64) for u in range(2)]
        x_codes = [gather_words(0)]
        for i in range(1, TILES):
            h_late.append(late.tile([P, PACK, P], F32, name="h_late%d" % i, offset=i * PIECE_BYTES))
            nc.sync.dma_start(h_late[i][:], h_view[1][:, :, i * P : (i + 1) * P])
        gen_weight = late.tile([P, TILES, 8], F32, name="gen_weight", offset=TILES * PIECE_BYTES)
        load_column(gen_weight, gen)
        halves = [
            interleave(h_early[:, :, 0:HALF], grouped_early[0][:], nc.vector.tensor_copy),
            interleave(h_early[:, :, HALF:V], grouped_early[1][:]),
        ]

        def first_pass(i, half):
            cols = slice((i % 2) * P, (i % 2 + 1) * P)
            multiply(i, 0, half[0][:, cols], half[1][:, cols], x_codes[0])

        def late_codes(i):
            grouped = keep.tile([P, P, PACK], BF16, name="grouped%d" % i, align_bytes=64)
            return quantize(interleave(h_late[i][:], grouped[:]), "%d" % i, keep.tile([P, P], U32, name="h_codes%d" % i, align_bytes=64))

        half = quantize(halves[0], "_half0", keep.tile([P, HALF], U32, name="h_codes_half0", align_bytes=64))
        first_pass(0, half)
        first_pass(1, half)
        half = quantize(halves[1], "_half1", keep.tile([P, HALF], U32, name="h_codes_half1", align_bytes=64))
        first_pass(2, half)
        first_pass(LAST, half)
        h_codes, h_scales = late_codes(0)
        x_codes.append(keep.tile([P, S], U32, name="x_codes1", align_bytes=64))
        for u in range(2):
            cols = slice(u * S // 2, (u + 1) * S // 2)
            entries = offs_list[:, u * S // 32 : (u + 1) * S // 32]
            nc.vector.tensor_copy(x_codes[1][:, cols], table_words[1][:].bitcast(U32).indirect(entries))
            nc.tensor.matmul_mx(
                out=banks[0][:, cols],
                lhsT=h_codes[:].bitcast(FP8X4),
                lhsT_scale=h_scales[:],
                rhs=x_codes[1][:, cols].bitcast(FP8X4),
                rhs_scale=planes[1][:, cols],
                start=False,
                stop=(u == 1),
            )

        def second_pass(i):
            h_codes, h_scales = late_codes(i)
            multiply(i, 1, h_codes[:], h_scales[:], x_codes[1])

        def held(shape, name, i):
            return late.tile(shape, F32, name=name, offset=i * PIECE_BYTES)

        maxima = {}

        def maximum(i, minus_max):
            nc.vector.tensor_reduce(minus_max[:], banks[i][:], mybir.AxisListType.X, ALU.max, negate=True)
            maxima[i] = minus_max

        totals, exps, factors = {}, {}, {}

        def exponentials(i, e):
            totals[i] = keep.tile([P, 1], F32, name="total%d" % i)
            nc.scalar.activation(e[:], banks[i][:], ACT.Exp, bias=maxima[i][:], accum_out=totals[i][:])
            exps[i] = e

        def factor(i):
            inverse = keep.tile([P, 1], F32, name="inverse%d" % i)
            nc.vector.reciprocal(inverse[:], totals[i][:])
            factors[i] = keep.tile([P, 1], F32, name="factor%d" % i)
            nc.scalar.activation(factors[i][:], inverse[:], ACT.Copy, scale=gen_weight[:, i, 0:1])

        def mix(i):
            width = S // 2 if i == LAST else S
            for first in range(0, S, width):
                cols = slice(first, first + width)
                mixed = keep.tile([P, width], F32, name="mixed%d_%d" % (i, first))
                nc.vector.scalar_tensor_tensor(mixed[:], exps[i][:, cols], factors[i][:], cp[i][:, cols], ALU.mult, ALU.add)
                nc.sync.dma_start(out[i * P : (i + 1) * P, cols], mixed[:])

        second_pass(1)
        maximum(0, held([P, 1], "minus_max0", 1))
        second_pass(2)
        maximum(1, held([P, 1], "minus_max1", 2))
        second_pass(LAST)
        exponentials(0, held([P, S], "exp0", LAST))
        exponentials(1, keep.tile([P, S], F32, name="exp1"))
        for i in range(2, TILES):
            maximum(i, keep.tile([P, 1], F32, name="minus_max%d" % i))
            exponentials(i, keep.tile([P, S], F32, name="exp%d" % i))
            factor(i - 2)
        for i in range(TILES):
            mix(i)
            if i + 2 < TILES:
                factor(i + 2)
